import numpy as np, ml_dtypes
CORES = [10,34,74,98]
N = 4
import mx_ref
BF = ml_dtypes.bfloat16
def pick(q, e):
    c = np.concatenate([q[0].reshape(128, -1, 4), np.zeros((128, 1, 4), np.uint8)], axis=1); s = np.concatenate([q[1], np.ones((16, 1), np.uint8)], axis=1)
    return (np.ascontiguousarray(c[:, e].reshape(128, -1)), np.ascontiguousarray(s[:, e]))
def join(*qs):
    return (np.concatenate([q[0] for q in qs], axis=1), np.concatenate([q[1] for q in qs], axis=1))
def put(q, e, v):
    c, s = q[0].reshape(128, -1, 4).copy(), q[1].copy(); c[:, e] = v[0].reshape(128, -1, 4); s[:, e] = v[1]
    return (c.reshape(128, -1), s)
def pk(c, s):
    return (np.ascontiguousarray(c), mx_ref.live(s))
def emit(q):
    return q[0], q[1]
def cols(t, e):
    v = np.concatenate([t.reshape(128, -1, 4), np.zeros((128, 1, 4), BF)], axis=1)
    return np.ascontiguousarray(v[:, e]).reshape(128, -1)
def tile(rs):
    return np.stack(rs, axis=2).reshape(128, -1).astype(BF)
def cut(t, i, w=512):
    return t[:, w * i:w * i + w]
def f(rng, *shape):
    return mx_ref.flush((rng.standard_normal(shape, dtype=np.float32) * np.exp2(rng.integers(-2, 3, shape[:-1] + (1,)))).astype(BF))
def wide(rng, *shape, cols=0):
    v = rng.standard_normal(shape, dtype=np.float32) * np.exp2(rng.integers(-12, 13, shape)).astype(np.float32)
    if cols: v *= np.repeat(np.exp2(rng.integers(-cols, cols + 1, shape[:-2] + (1, shape[-1] // 4))) * (rng.random(shape[:-2] + (1, shape[-1] // 4)) > 0.0625), 4, axis=-1).astype(np.float32)
    return mx_ref.flush(v.astype(BF))
T, CAPP, CB, DF = 192, 80, 32, 80
LEVELS = np.array([0, 16, 32, 64], np.float32)
def taken(first, a):
    return np.concatenate([s * T + np.flatnonzero(first[s] == a)[:CAPP] for s in range(N)])
def plain(rng):
    rt, r2 = np.array(f(rng, 128, 512)), np.zeros((128, 512), BF)
    rt[:, 4 * N:] = 0
    v = f(rng, 128, 4 * N + 4).astype(np.float32).reshape(128, N + 1, 4)
    v = v - np.mean(v, axis=(0, 2), keepdims=True)
    r2[:, :4 * N + 4] = mx_ref.flush(v.reshape(128, -1).astype(BF))
    return {"x": np.array(f(rng, N, 128, 4 * T)), "rt": np.stack([rt] * N), "w": np.array(f(rng, N, 128, 2048)), "r2": np.stack([r2] * N), "vx": f(rng, N, 128, 512), "vh": f(rng, N, 128, 512)}
def planned(rng, A, B, V, dead=None, same=False):
    d = plain(rng)
    rt, r2, wt = d["rt"], d["r2"], d["w"].reshape(N, 128, 4, 128, 4)
    rt[:, 120:] = 0
    r2[:, :4 * N + 4] = 0
    wt[:, 120:] = 0
    for k in range(N + 1):
        r2[:, 4 * k:4 * k + 4, 4 * k:4 * k + 4] = 32
        wt[:, 120 + k // 4, :, 4 * k:4 * k + 4, k % 4] = 64
    k = N + 1
    wt[:, 120 + k // 4, :, :, k % 4] = -64
    if same:
        p = f(rng, 128, 4 * N)
        x = np.stack([cols(p, A[s]) for s in range(N)])
    else: x = f(rng, N, 128, 4 * T)
    x = np.array(x, np.float32).reshape(N, 128, T, 4)
    g = rt[0].astype(np.float32).reshape(128, 128, 4)
    for s in range(N): x[s] = x[s] + g[:, A[s]]
    x[:, 120:] = 0
    s, j = np.nonzero(B >= 0)
    b = B[s, j]
    x[s, 120 + b // 4, j, b % 4] = 64
    x[:, 120 + N // 4, :, N % 4] = LEVELS[V]
    if dead is not None: x[:, 120 + k // 4, :, k % 4] = np.where(dead, 256, 0)
    d["x"] = np.array(mx_ref.flush(x.reshape(N, 128, 4 * T).astype(BF)))
    return d
def choose(rng, A):
    B, V = (A + 1 + rng.integers(0, N - 1, A.shape)) % N, np.zeros((N, T), int)
    for a in range(N):
        k = taken(A, a)
        V.flat[k] = 3
        k = rng.permutation(k)[:DF]
        V.flat[k] = 0
        B.flat[k] = np.resize(rng.permutation([b for b in range(N) if b != a]), len(k))
    return B, V
def setup_inputs(rng):
    return plain(rng)
def setup_inputs_crowd(rng):
    h, A = int(rng.integers(1, N - 1)), []
    o = (int(rng.choice([i for i in range(1, N) if i not in (h, h + 1)])), h)
    for s in range(N):
        one, two, e = (s + o[0]) % N, (s + o[1]) % N, int(rng.integers(1, 9))
        rest = [a for a in range(N) if a not in (one, two, (two + 1) % N)]
        A.append(rng.permutation(np.concatenate([np.full(CAPP, one), np.full(CAPP + e, two), np.resize(rng.permutation(rest), T - 2 * CAPP - e)])))
    A = np.stack(A)
    B, V = choose(rng, A)
    for a in range(N):
        one, two, e = (a + o[0]) % N, (a + o[1]) % N, int(rng.integers(1, CB // 4 + 1))
        rest = [b for b in range(N) if b not in (a, one, two)]
        k = taken(A, a)
        k = rng.permutation(k[V.reshape(-1)[k] == 0])
        B.flat[k] = np.concatenate([np.full(CB, one), np.full(CB + e, two), np.resize(rng.permutation(rest), len(k) - 2 * CB - e)])
    return planned(rng, A, B, V)
def setup_inputs_few(rng):
    none, less, even, full = rng.permutation(N)[:4]
    act, n = [a for a in range(N) if a not in (none, less, even, full)] or [full], DF // (2 * N)
    fix = np.concatenate([np.full(n, less), np.full(2 * n, even), np.full(CAPP + 4, full)])
    A = np.stack([rng.permutation(np.concatenate([fix, np.resize(rng.permutation(act), T - len(fix))])) for s in range(N)])
    B, V = choose(rng, A)
    m = (A == less) | (A == even)
    V[m] = rng.integers(0, 4, int(np.count_nonzero(m)))
    k = taken(A, full)
    V.flat[k] = 3
    k = np.concatenate([k[-16::5], rng.permutation(k[:-16])[:DF - 4]])
    V.flat[k] = 0
    B.flat[k] = np.resize(rng.permutation([b for b in range(N) if b != full]), DF)
    d = planned(rng, A, B, V)
    p, t = 120 + (N + 2) // 4, (N + 2) % 4
    d["x"][:, p, t::4] = 64
    d["w"].reshape(N, 128, 4, 128, 4)[:, p, :, 4 * N + 4:4 * N + 8, t] = 64
    d["r2"][:, 4 * N + 4:4 * N + 8] = 0
    d["r2"][:, 4 * N + 4:4 * N + 8, :4 * N] = -64
    d["x"] = (d["x"].astype(np.float32) * np.float32(2.0 ** 21)).astype(BF)
    d["r2"] = (d["r2"].astype(np.float32) * np.float32(2.0 ** 24)).astype(BF)
    return d
def setup_inputs_ties(rng):
    lo, hi = np.sort(rng.permutation(N)[:2])
    k = int(rng.choice([i for i in range(N - 1) if i != hi]))
    act = [a for a in range(N) if a != hi]
    A = np.stack([rng.permutation(np.resize(rng.permutation(act), T)) for s in range(N)])
    B, V, c = np.zeros((N, T), int), np.full((N, T), 3), 3 * (DF // 6)
    for a in act:
        g = rng.permutation(taken(A, a))
        n = (len(g) - 2 * c) // 3
        B.flat[g] = (a + 1) % N
        V.flat[g[:c]] = 0
        B.flat[g[c:2 * c]] = (a + 2) % N
        V.flat[g[c:2 * c]] = 1
        B.flat[g[2 * c:2 * c + 3 * n]] = (a + 3 + np.repeat(np.arange(n), 3) % (N - 3)) % N
        V.flat[g[2 * c:2 * c + 3 * n]] = 2
    d = planned(rng, A, B, V, same=True)
    d["rt"][:, :, 4 * hi:4 * hi + 4] = d["rt"][:, :, 4 * lo:4 * lo + 4]
    d["r2"][:, 4 * k + 4:4 * k + 8, 4 * k:4 * k + 4] = 32
    d["r2"][:, :, 4 * k + 4:4 * k + 8] = d["r2"][:, :, 4 * k:4 * k + 4]
    return d
def setup_inputs_zero(rng):
    A = np.stack([rng.permutation(np.resize(np.arange(N), T)) for s in range(N)])
    B, V, dead = (A + 1 + rng.integers(0, N - 1, A.shape)) % N, np.full((N, T), 3), np.zeros((N, T), bool)
    for a in range(N):
        k = rng.permutation(taken(A, a))
        z = DF // 2 if a % 2 else DF + DF // 8
        dead.flat[k[:z]] = True
        B.flat[k[:z]] = -1
        V.flat[k[:z]] = 0
        g = k[z:DF]
        if len(g):
            V.flat[g] = 1
            B.flat[g] = np.resize(rng.permutation([b for b in range(N) if b != a]), len(g))
        if a == 0: blank = k[:z:2]
    d = planned(rng, A, B, V, dead=dead)
    nil = np.where(d["rt"][0, :, :4].astype(np.float32) < 0, np.float32(0.0), np.float32(-0.0)).astype(BF)
    for i in blank: d["x"][i // T, :, 4 * (i % T):4 * (i % T) + 4] = nil
    return d
def setup_inputs_spread(rng):
    return {**plain(rng), "x": wide(rng, N, 128, 4 * T, cols=4)}
def check_inputs(d):
    b = []
    for k in ("x", "rt", "w", "r2", "vx", "vh"):
        v = np.abs(d[k].astype(np.float32))
        if not (np.isfinite(v).all() and ((v == 0) | (v >= 2.0 ** -30) & (v <= 2.0 ** 30)).all()): b.append("a value of " + k)
    for k, n in (("rt", N), ("r2", N + 1)):
        v = d[k].astype(np.float32)
        if (v[:, :, 4 * n:] != 0).any(): b.append(k + " has numbers behind its first columns")
        if (v != v[:1]).any(): b.append(k + " differs between ranks")
    return b
def reference(x, rt, w, r2, vx, vh):
    q = [mx_ref.quantize(np.ascontiguousarray(x[s])) for s in range(N)]
    every = join(*q)
    first = np.stack([np.argmax(mx_ref.matmul(mx_ref.quantize(np.ascontiguousarray(rt[s])), q[s])[:N] + np.float32(0.0), axis=0) for s in range(N)])
    who, at, made = np.full((N, N * CB), -1), np.full((N, N * CB), -1), []
    for a in range(N):
        k = taken(first, a)
        t = pick(every, np.concatenate([k, np.full(N * CAPP - len(k), -1)]))
        z = [mx_ref.matmul(mx_ref.quantize(np.ascontiguousarray(cut(w[a], i))), t) for i in range(4)]
        h = mx_ref.quantize(np.ascontiguousarray(tile([np.maximum(v, np.float32(0.0)) * np.float32(0.0625) for v in z])))
        made.append(h)
        e = mx_ref.matmul(mx_ref.quantize(np.ascontiguousarray(r2[a])), h)[:N + 1, :len(k)] + np.float32(0.0)
        late = np.sort(np.argsort(e[N], kind="stable")[:DF])
        e[a] = -np.inf
        second = np.argmax(e[:N], axis=0)
        for b in range(N):
            m = late[second[late] == b][:CB]
            who[b, a * CB:a * CB + len(m)] = k[m]
            at[b, a * CB:a * CB + len(m)] = a * N * CAPP + m
    made = join(*made)
    y, oc, osc = np.zeros((N, 128, N * CB), np.float32), np.zeros((N, 128, 4 * N * CB), np.uint8), np.zeros((N, 16, N * CB), np.uint8)
    for b in range(N):
        t, h = pick(every, who[b]), pick(made, at[b])
        v = mx_ref.matmul(mx_ref.quantize(np.ascontiguousarray(vx[b])), t) + mx_ref.matmul(mx_ref.quantize(np.ascontiguousarray(vh[b])), h)
        y[b] = np.where(who[b] >= 0, v, np.float32(0.0))
        oc[b], osc[b] = emit(h)
    return {"y": y, "who": who.astype(np.float32).reshape(N, 1, N * CB), "oc": oc, "osc": osc}

@@ -1,0 +1,328 @@
+from concourse.bass import DstId, RemoteDMATransfer
+from concourse.mybir import dt, AluOpType as OP, AxisListType, ActivationFunctionType as AF
+
+N, TOK, CAP, CB, DF = 4, 192, 80, 32, 80
+NX = N * CAP
+XC = 336
+HB = 352
+EPS, DEL, BIG, LOW = 1e-30, 1e-31, 1e29, -9e29
+RTB = [0, 1, 2, 3, 6, 7, 4, 5, 4, 7, 6, 5, 4]
+RTS = [7, 4, 9]
+
+SCRATCH = {
+    "rtt": ("sbuf", [128, 512], "bfloat16"), "rtq": ("sbuf", [128, 128], "float8_e4m3fn_x4"), "rts": ("sbuf", [128, 128], "uint8"),
+    "rpq": ("sbuf", [128, 416], "float8_e4m3fn_x4"), "rps": ("sbuf", [128, 416], "uint8"), "rto": ("sbuf", [128, 26], "uint16"),
+    "xt": ("sbuf", [128, 776], "bfloat16"), "xq": ("sbuf", [128, 194], "float8_e4m3fn_x4"), "xs": ("sbuf", [128, 194], "uint8"),
+    "wt": ("sbuf", [128, 2048], "bfloat16"), "wq": ("sbuf", [128, 512], "float8_e4m3fn_x4"), "wsc": ("sbuf", [128, 512], "uint8"),
+    "r2t": ("sbuf", [128, 512], "bfloat16"), "r2q": ("sbuf", [128, 128], "float8_e4m3fn_x4"), "r2s": ("sbuf", [128, 128], "uint8"),
+    "r2p": ("sbuf", [128, 512], "float8_e4m3fn_x4"), "r2ps": ("sbuf", [128, 512], "uint8"), "r2o": ("sbuf", [128, 32], "uint16"),
+    "vxt": ("sbuf", [128, 512], "bfloat16"), "vxq": ("sbuf", [128, 128], "float8_e4m3fn_x4"), "vxs": ("sbuf", [128, 128], "uint8"),
+    "vht": ("sbuf", [128, 512], "bfloat16"), "vhq": ("sbuf", [128, 128], "float8_e4m3fn_x4"), "vhs": ("sbuf", [128, 128], "uint8"),
+    "hb": ("sbuf", [128, 4 * (NX + 2)], "bfloat16"),
+    "sl1": ("sbuf", [128, 240], "float8_e4m3fn_x4"), "ss1": ("sbuf", [128, 240], "uint8"),
+    "land1": ("sbuf", [128, XC], "float8_e4m3fn_x4"), "lans1": ("sbuf", [128, XC], "uint8"),
+    "msgo": ("sbuf", [128, 32], "bfloat16"), "msgi": ("sbuf", [128, 32], "bfloat16"),
+    "xw": ("sbuf", [128, 704], "float8_e4m3fn_x4"), "xws": ("sbuf", [128, 704], "uint8"),
+    "sl2": ("sbuf", [128, 192], "float8_e4m3fn_x4"), "ss2": ("sbuf", [128, 192], "uint8"),
+    "land2": ("sbuf", [128, 256], "float8_e4m3fn_x4"), "lans2": ("sbuf", [128, 256], "uint8"),
+    "fin": ("sbuf", [128, 256], "float8_e4m3fn_x4"), "fins": ("sbuf", [128, 256], "uint8"),
+    "lwho": ("sbuf", [128, 32], "float32"), "whot": ("sbuf", [128, 32], "float32"),
+    "z1": ("sbuf", [128, 192], "float32"), "z2": ("sbuf", [128, 192], "float32"), "z3": ("sbuf", [128, 192], "float32"),
+    "mk": ("sbuf", [128, 192], "bfloat16"), "cum": ("sbuf", [128, 192], "bfloat16"), "zb": ("sbuf", [128, 320], "bfloat16"), "zf": ("sbuf", [128, 320], "float32"),
+    "jka": ("sbuf", [128, 1152], "bfloat16"), "jkd": ("sbuf", [128, 512], "bfloat16"),
+    "cnt1": ("sbuf", [128, 8], "float32"), "cntm": ("sbuf", [128, 4], "float32"), "off1": ("sbuf", [128, 24], "uint16"), "ozero": ("sbuf", [128, 4], "uint16"),
+    "inv": ("sbuf", [128, 320], "float32"), "em": ("sbuf", [128, 320], "float32"), "emb": ("sbuf", [128, 320], "float32"),
+    "y1": ("sbuf", [128, 320], "float32"), "y2": ("sbuf", [128, 320], "float32"), "ns": ("sbuf", [128, 320], "float32"),
+    "gd": ("sbuf", [128, 320], "float32"), "nq": ("sbuf", [128, 320], "float32"), "dp": ("sbuf", [128, 320], "float32"),
+    "mk2": ("sbuf", [128, 320], "bfloat16"), "cum2": ("sbuf", [128, 320], "bfloat16"),
+    "jk2": ("sbuf", [128, 960], "bfloat16"), "jkb": ("sbuf", [128, 960], "bfloat16"), "jke": ("sbuf", [128, 336], "bfloat16"),
+    "en": ("sbuf", [128, 4], "float32"), "lt": ("sbuf", [128, 4], "float32"), "pen": ("sbuf", [128, 4], "float32"),
+    "c1": ("sbuf", [128, 4], "float32"), "c2": ("sbuf", [128, 4], "float32"), "cc": ("sbuf", [128, 2], "float32"),
+    "bc": ("sbuf", [128, 64], "float32"), "bt": ("sbuf", [128, 64], "float32"), "qm": ("sbuf", [128, 2], "float32"),
+    "g4": ("sbuf", [128, 8], "float32"), "tl": ("sbuf", [128, 2], "float32"), "ini": ("sbuf", [128, 1], "float32"),
+    "cnt2": ("sbuf", [128, 4], "float32"), "off2": ("sbuf", [128, 12], "uint16"),
+    "nb": ("sbuf", [128, 320], "bfloat16"), "num": ("sbuf", [128, XC], "float32"), "wg": ("sbuf", [128, 96], "float32"), "wtr": ("sbuf", [128, 96], "float32"),
+    "ys": ("sbuf", [128, 128], "float32"),
+    "th1": ("sbuf", [128, 1], "float32"), "eb1": ("sbuf", [128, 1], "float32"), "th2": ("sbuf", [128, 1], "float32"), "eb2": ("sbuf", [128, 1], "float32"),
+    "pI": ("sbuf", [128, 16], "int32"), "rI": ("sbuf", [128, 16], "int32"), "qI": ("sbuf", [128, 16], "int32"),
+    "b16": ("sbuf", [128, 8], "int32"), "b32": ("sbuf", [128, 8], "int32"), "bfin": ("sbuf", [128, 16], "int32"), "ofi": ("sbuf", [128, 16], "int32"),
+    "cs": ("sbuf", [128, 8], "float32"), "csp": ("sbuf", [128, 8], "float32"), "csn": ("sbuf", [128, 8], "float32"), "cm": ("sbuf", [128, 8], "float32"), "cmn": ("sbuf", [128, 8], "float32"),
+    "i80": ("sbuf", [128, 80], "float32"), "ofin": ("sbuf", [128, 16], "uint16"),
+    "ps": ("psum", [128, 4096], "float32"),
+}
+SEMAPHORES = ["v", "a", "t", "gq", "dx", "drt", "dw", "dr2", "dvx", "dvh", "dxw", "dnb", "dout", "ls",
+              "arr0", "arr1", "arr2", "arr3", "am", "arrb", "aw"]
+
+
+def rank_program(g, core, T, topo):
+    rank = T.rank_of(core)
+    if rank is None:
+        return
+    cores = list(T.cores)
+    me_chip = topo.chip(core)
+    others = [(rank + 1 + k) % N for k in range(N - 1)]
+    order = [b for b in others if not topo.same_plane(topo.chip(cores[b]), me_chip)] + \
+            [b for b in others if topo.same_plane(topo.chip(cores[b]), me_chip)]
+    eng = {"v": g.vector, "a": g.scalar, "t": g.tensor, "s": g.sync, "g": g}
+    semof = {"v": "v", "a": "a", "t": "t", "g": "gq"}
+    tot, seen = {}, {q: {} for q in eng}
+
+    def wait(q, deps):
+        for s, n in deps:
+            if seen[q].get(s, 0) < n:
+                eng[q].wait_ge(T.sem[s], n)
+                seen[q][s] = n
+
+    def op(q, fn, *deps):
+        wait(q, deps)
+        s = semof[q]
+        fn(eng[q]).then_inc(T.sem[s], 1)
+        tot[s] = tot.get(s, 0) + 1
+        return (s, tot[s])
+
+    def dma(q, s, out, src, *deps):
+        wait(q, deps)
+        eng[q].dma_start(out, src).then_inc(T.sem[s], 16)
+        tot[s] = tot.get(s, 0) + 16
+        return (s, tot[s])
+
+    def send(b, out, src, sem, *deps):
+        wait("g", deps)
+        rid, pid, _ = topo.addr(cores[b])
+        g.remote_dma(out, src, T.sem[sem], T.sem.ls, pid, rid, topo.mask(core, cores[b]))
+        tot["ls"] = tot.get("ls", 0) + len(topo.engines(core, cores[b]))
+
+    def arrivals(srcs, per):
+        return per * sum(len(topo.engines(cores[s], core)) for s in srcs)
+
+    u8, u32 = dt.uint8, dt.uint32
+    c8 = lambda v: v.bitcast(u8)
+    ms = lambda ap, val, *d: op("v", lambda e: e.memset(ap, val), *d)
+    ts = lambda out, x, s1, s2, o0, o1, *d: op("v", lambda e: e.tensor_scalar(out, x, s1, s2, o0) if o1 is None else e.tensor_scalar(out, x, s1, s2, o0, o1), *d)
+    tt = lambda out, x, y, o, *d: op("v", lambda e: e.tensor_tensor(out, x, y, o), *d)
+    cp = lambda out, x, *d: op("v", lambda e: e.tensor_copy(out, x), *d)
+    red = lambda out, x, o, *d: op("v", lambda e: e.tensor_reduce(out, x, AxisListType.X, o), *d)
+    scan = lambda out, x, y, i, *d: op("v", lambda e: e.tensor_tensor_scan(out, x, y, i, OP.add, OP.add), *d)
+    quant = lambda q, s, x, *d: op("v", lambda e: e.quantize_mx(q, s, x), *d)
+    act = lambda out, x, f, b, s, *d: op("a", lambda e: e.activation(out, x, f, bias=b, scale=s), *d)
+    acc = lambda out, x, f, b, o, *d: op("a", lambda e: e.activation(out, x, f, bias=b, scale=1.0, accum_out=o), *d)
+    pickq = lambda out, win, off, *d: op("v", lambda e: e.tensor_copy(out.bitcast(u32), win.bitcast(u32).indirect(off)), *d)
+    picks = lambda out, win, off, *d: op("a", lambda e: e.activation(out, win.indirect(off), AF.Copy), *d)
+    quad = lambda q: slice(32 * q, 32 * q + 32)
+    bank = lambda k, n: T.ps[:, 512 * k:512 * k + n]
+
+    def mm(out, w, ws, x, xs, start, stop, *d):
+        return op("t", lambda e: e.matmul_mx(out, w, ws, x, xs, start, stop), *d)
+
+    d_rt = dma("a", "drt", T.rtt[:, 0:16], T.rt[:, 0:16])
+    d_x = dma("s", "dx", T.xt[:, 0:768], T.x[:])
+    d_w = dma("s", "dw", T.wt[:], T.w[:], d_x)
+    d_r2 = dma("s", "dr2", T.r2t[:, 0:20], T.r2[:, 0:20])
+    d_vx = dma("s", "dvx", T.vxt[:], T.vx[:])
+    d_vh = dma("s", "dvh", T.vht[:], T.vh[:])
+
+    gi = lambda out, pat, cmul: op("g", lambda e: e.iota(out, pat, 0, cmul))
+    gi(T.pI[:], [[0, 16]], 1)
+    gi(T.b16[:], [[16, 8]], 0)
+    k_g = gi(T.b32[:], [[32, 8]], 0)
+    k_fin = gi(T.bfin[:], [[32, 2], [64, 4], [16, 2]], 0)
+    k_80 = op("g", lambda e: e.iota(T.i80[:], [[1, 80]], 0, 0, allow_small_or_imprecise_dtypes=True))
+    ms(T.rtt[:, 32:512], 0.0)
+    c = 0
+    while c < 13:
+        k_rto = ms(T.rto[:, 2 * c:2 * c + 2], RTB[c])
+        c += 1
+    k_x0 = ms(T.xt[:, 768:776], 0.0)
+    ms(T.th1[0:64, :], -EPS / 2)
+    ms(T.th1[64:128, :], EPS / 2)
+    ms(T.eb1[0:32, :], 0.0)
+    ms(T.eb1[32:64, :], -EPS)
+    ms(T.eb1[64:96, :], EPS)
+    k_th = ms(T.eb1[96:128, :], 0.0)
+    ms(T.zb[:], 0.0)
+    k_jk = ms(T.jkd[:, 192:193], -192.0)
+    k_jk = ms(T.jkd[:, 448:449], -192.0)
+    kr = ts(T.rI[:], T.pI[:], 15, None, OP.bitwise_and, None, k_g)
+    kq = ts(T.qI[:], T.pI[:], 31, None, OP.bitwise_and, None)
+    k1 = tt(T.cs[:], T.rI[:, 0:8], T.b16[:], OP.add, kr)
+    ts(T.csp[:], T.cs[:], 0.5, None, OP.add, None, k1)
+    k_cs = ts(T.csn[:], T.cs[:], -1.0, -0.5, OP.mult, OP.add)
+    k_lw = ms(T.lwho[:], -1.0)
+    k_mi = ms(T.msgi[:, 8 * rank:8 * rank + 8], 0.0)
+    k_mo = ms(T.msgo[:], 0.0)
+
+    k = ts(T.rtt[:, 16:32], T.rtt[:, 0:16], -1.0, None, OP.mult, None, d_rt)
+    k_rq = quant(T.rtq[:], T.rts[:], T.rtt[:], k)
+    k_rp = pickq(T.rpq[:], T.rtq[:], T.rto[:], k_rq)
+    k_rs = picks(T.rps[:], T.rts[:], T.rto[:], k_rq, k_rto)
+    k_xq = quant(T.xq[:], T.xs[:], T.xt[:], d_x, k_x0)
+    dm = []
+    for j in range(3):
+        mm(bank(j, 192), T.rpq[:, 0:128], T.rps[:, 0:128], T.xq[:, 0:192], T.xs[:, 0:192], True, False, k_rp, k_rs, k_xq)
+        a = 32 * RTS[j]
+        dm.append(mm(bank(j, 192), T.rpq[:, a:a + 128], T.rps[:, a:a + 128], T.xq[:, 0:192], T.xs[:, 0:192], False, True))
+    k_z1 = act(T.z1[:], bank(0, 192), AF.Identity, T.eb1[:], 1.0, dm[0], k_th)
+    ms(T.jke[:, 320:321], -320.0)
+    ms(T.ozero[:], TOK)
+    k2 = tt(T.cm[:], T.qI[:, 0:8], T.b32[:], OP.add, kq)
+    k_cm = ts(T.cmn[:], T.cm[:], -1.0, -0.5, OP.mult, OP.add, k2)
+    k = tt(T.z2[:], bank(1, 192), T.z1[:], OP.min, dm[1], k_z1)
+    k_d1 = tt(T.z3[:], bank(2, 192), T.z2[:], OP.min, dm[2], k)
+    k = ts(T.mk[:], T.z3[:], T.th1[:], None, OP.is_gt, None, k_d1)
+    k_cum = scan(T.cum[:], T.mk[:], T.zb[:, 0:192], 0.0, k)
+    k_a = [acc(T.jka[:, 192 * c:192 * c + 192], T.cum[:], AF.Sign, T.csn[:, c:c + 1], T.cnt1[:, c:c + 1], k_cum, k_cs) for c in range(3)]
+    k3 = ts(T.jkd[:, 0:192], T.cum[:], T.csp[:, 3:4], 2.0, OP.is_gt, OP.mult, k_cum)
+    k4 = ts(T.jkd[:, 256:448], T.cum[:], T.csp[:, 4:5], 2.0, OP.is_gt, OP.mult)
+    ts(T.cnt1[:, 5:6], T.cum[:, 191:192], -2.0, 192.0, OP.mult, OP.add)
+    red(T.cnt1[:, 3:4], T.jkd[:, 0:193], OP.add, k3, k_jk)
+    k_c = red(T.cnt1[:, 4:5], T.jkd[:, 256:449], OP.add, k4)
+    pk, psc, k_off = {}, {}, {}
+    for i, b in enumerate(order + [rank]):
+        for q in range(N):
+            k_off[b] = ts(T.off1[quad(q), 6 * b:6 * b + 6], T.cnt1[quad(b), 0:6], -0.5, 96.0, OP.mult, OP.add, k_c, k_a[-1])
+        o, so = (T.sl1[:, 80 * i:80 * i + 80], T.ss1[:, 80 * i:80 * i + 80]) if b != rank else \
+                (T.land1[:, 80 * b:80 * b + 80], T.lans1[:, 80 * b:80 * b + 80])
+        pk[b] = pickq(o, T.xq[:, 0:194], T.off1[:, 6 * b:6 * b + 5], k_off[b])
+        psc[b] = picks(so, T.xs[:, 0:194], T.off1[:, 6 * b:6 * b + 5], k_off[b])
+        if b != rank:
+            send(b, c8(T.land1[:, 80 * rank:80 * rank + 80]), c8(T.sl1[:, 80 * i:80 * i + 80]), "arr%d" % rank, pk[b], k_lw)
+            send(b, T.lans1[:, 80 * rank:80 * rank + 80], T.ss1[:, 80 * i:80 * i + 80], "arr%d" % rank, psc[b])
+    k_m = [acc(T.jka[:, 576 + 192 * c:768 + 192 * c], T.cum[:], AF.Sign, T.cmn[:, c:c + 1], T.cntm[:, c:c + 1], k_cm) for c in range(3)]
+    m_v, m_a = {}, {}
+    for b in order + [rank]:
+        m, o = (T.msgo, 8 * b) if b != rank else (T.msgi, 8 * rank)
+        m_v[b] = cp(m[:, o + 1:o + 2], T.off1[:, 6 * b + 5:6 * b + 6], k_off[b], k_mo)
+        for c in range(3):
+            m_a[b] = act(m[quad(c), o:o + 1], T.cntm[quad(b), c:c + 1], AF.Copy, 96.0, -0.5, k_m[2], k_mo)
+        if b != rank:
+            send(b, T.msgi[:, 8 * rank:8 * rank + 2], T.msgo[:, o:o + 2], "am", m_v[b], m_a[b])
+
+    k_z = pickq(T.land1[:, NX:XC], T.xq[:, 0:194], T.ozero[:, 0:1], k_xq)
+    k_zs = picks(T.lans1[:, NX:XC], T.xs[:, 0:194], T.ozero[:, 0:1], k_z)
+    k_wq = quant(T.wq[:], T.wsc[:], T.wt[:], d_w)
+    ms(T.r2t[:, 40:512], 0.0)
+    k = ts(T.r2t[:, 20:40], T.r2t[:, 0:20], -1.0, None, OP.mult, None, d_r2)
+    k_r2q = quant(T.r2q[:], T.r2s[:], T.r2t[:], k)
+    srt = sorted(others)
+    one = {srt[0]: srt[1], srt[1]: srt[0], srt[2]: srt[0], rank: 0}
+    two = {srt[0]: srt[2], srt[1]: srt[2], srt[2]: srt[1], rank: 0}
+    blocks = [0, 1, 2, 3] + [5 + one[q] for q in range(N)] + [5 + two[q] for q in range(N)] + [4] * 4
+    for c in range(16):
+        k_o = ms(T.r2o[:, 2 * c:2 * c + 2], blocks[c])
+    k_r2p = pickq(T.r2p[:], T.r2q[:], T.r2o[:], k_o, k_r2q)
+    k_r2s = picks(T.r2ps[:], T.r2s[:], T.r2o[:], k_o, k_r2q)
+    k_z2 = pickq(T.land2[:, 64 * rank:64 * rank + 64], T.xq[:, 0:194], T.ozero[:], k_xq)
+    k_z2s = picks(T.lans2[:, 64 * rank:64 * rank + 64], T.xs[:, 0:194], T.ozero[:], k_z2)
+    k_vx = quant(T.vxq[:], T.vxs[:], T.vxt[:], d_vx)
+    k_vh = quant(T.vhq[:], T.vhs[:], T.vht[:], d_vh)
+    for q in range(N):
+        ms(T.th2[quad(q), :], EPS / 2 if q == srt[2] else -EPS / 2)
+        k_t2 = ms(T.eb2[quad(q), :], -EPS if q == srt[1] else 0.0)
+    ms(T.zf[:], 0.0)
+    k_num = ms(T.num[:], -1.0)
+    k = tt(T.ofi[:], T.rI[:], T.bfin[:], OP.add, k_fin)
+    k_ofin = cp(T.ofin[:], T.ofi[:], k)
+
+    arr = lambda s: ("arr%d" % s, arrivals([s], 2))
+    home = (pk[rank], psc[rank])
+    halves = [(0, 160, [0, 1]), (160, NX + 2, [2, 3])]
+    kq_h = []
+    for h, (c0, c1, who) in enumerate(halves):
+        deps = [arr(s) for s in who if s != rank] + list(home) + [k_z, k_zs, k_wq, k_d1, k_z1]
+        w = [mm(bank(4 * h + i, c1 - c0), T.wq[:, 128 * i:128 * i + 128], T.wsc[:, 128 * i:128 * i + 128], T.land1[:, c0:c1], T.lans1[:, c0:c1], True, True, *deps) for i in range(4)]
+        hv = lambda i: T.hb[:, 4 * c0 + i:4 * c1:4]
+        k0 = act(hv(0), bank(4 * h, c1 - c0), AF.Relu, 0.0, 0.0625, w[0])
+        k1 = ts(hv(1), bank(4 * h + 1, c1 - c0), 0.0, 0.0625, OP.max, OP.mult, w[1])
+        k2 = act(hv(2), bank(4 * h + 2, c1 - c0), AF.Relu, 0.0, 0.0625, w[2])
+        k3 = ts(hv(3), bank(4 * h + 3, c1 - c0), 0.0, 0.0625, OP.max, OP.mult, w[3])
+        kq_h.append(quant(T.xw[:, HB + c0:HB + c1], T.xws[:, HB + c0:HB + c1], T.hb[:, 4 * c0:4 * c1], k0, k1, k2, k3))
+    alla = [arr(s) for s in range(N) if s != rank]
+    dma("s", "dxw", c8(T.xw[:, 0:XC]), c8(T.land1[:]), *alla, *home, k_z, k_zs)
+    d_xw = dma("s", "dxw", T.xws[:, 0:XC], T.lans1[:])
+    am = ("am", arrivals(others, 1))
+    for s in range(N):
+        d_nb = dma("s", "dnb", T.nb[0:1, 80 * s:80 * s + 80], T.msgi[0:80, 8 * s:8 * s + 1], am, m_v[rank], m_a[rank])
+
+    H = lambda a, b: (T.xw[:, HB + a:HB + b], T.xws[:, HB + a:HB + b])
+    P = lambda k: (T.r2p[:, 128 * k:128 * k + 128], T.r2ps[:, 128 * k:128 * k + 128])
+    e0 = mm(bank(1, 128), *H(0, 128), T.r2q[:], T.r2s[:], True, True, kq_h[0], k_r2p, k_r2s, k_r2q)
+    t_e = mm(bank(0, NX), *P(3), *H(0, NX), True, True, kq_h[1])
+    e1 = mm(bank(2, 128), *H(128, 256), T.r2q[:], T.r2s[:], True, True)
+    e2 = mm(bank(3, 128), *H(192, 320), T.r2q[:], T.r2s[:], True, True)
+    mm(bank(4, NX), *P(0), *H(0, NX), True, False)
+    f1 = mm(bank(4, NX), *P(1), *H(0, NX), False, True)
+    mm(bank(5, NX), *P(0), *H(0, NX), True, False)
+    f2 = mm(bank(5, NX), *P(2), *H(0, NX), False, True)
+    ken = [act(T.en[:, k:k + 1], T.ps[:, 512 * (k + 1) + 4:512 * (k + 1) + 5], AF.Copy, 0.0, 1.0, e) for k, e in enumerate((e0, e1, e2))]
+    for s in range(N):
+        ki = ts(T.inv[:, 80 * s:80 * s + 80], T.i80[:], T.msgi[:, 8 * s + 1:8 * s + 2], BIG, OP.is_ge, OP.mult, k_80, am, m_v[rank])
+    k_em = tt(T.em[:], bank(0, NX), T.inv[:], OP.add, t_e, ki)
+    kl = []
+    for k in range(3):
+        kc = ts(T.jk2[:, 320 * k:320 * k + 320], T.em[:], T.en[:, k:k + 1], None, OP.is_lt, None, k_em, ken[k])
+        if k < 2:
+            kl.append(acc(T.jkb[:, 320 * k:320 * k + 320], T.jk2[:, 320 * k:320 * k + 320], AF.Copy, 0.0, T.lt[:, k:k + 1], kc))
+        else:
+            kl.append(red(T.lt[:, k:k + 1], T.jk2[:, 320 * k:320 * k + 320], OP.add, kc))
+    k_y1 = act(T.y1[:], bank(4, NX), AF.Identity, T.eb2[:], 1.0, f1, k_t2)
+    for s in range(N):
+        k_n = act(T.num[0:1, 80 * s:80 * s + 80], T.nb[0:1, 80 * s:80 * s + 80], AF.Copy, float(TOK * s), 1.0, d_nb, k_num)
+    kp = ts(T.pen[:, 0:3], T.lt[:, 0:3], DF - 0.5, LOW, OP.is_ge, OP.mult, *kl)
+    k_y2 = tt(T.y2[:], bank(5, NX), T.y1[:], OP.min, f2, k_y1)
+    tt(T.c1[:, 0:3], T.en[:, 0:3], T.pen[:, 0:3], OP.add, kp)
+    kc = tt(T.c2[:, 0:3], T.lt[:, 0:3], T.pen[:, 0:3], OP.add)
+    k_ns = ts(T.ns[:], T.y2[:], T.th2[:], BIG, OP.is_le, OP.mult, k_y2)
+    red(T.cc[:, 0:1], T.c1[:, 0:3], OP.max, kc)
+    kc = red(T.cc[:, 1:2], T.c2[:, 0:3], OP.max)
+    k_eb = tt(T.emb[:], T.em[:], T.ns[:], OP.add, k_ns)
+    ts(T.bc[:, 0:32], T.zf[:, 0:32], T.cc[:, 0:1], None, OP.add, None, kc)
+    kc = ts(T.bc[:, 32:64], T.zf[:, 0:32], T.cc[:, 1:2], None, OP.add, None)
+    kc = op("v", lambda e: e.transpose(T.bt[:], T.bc[:]), kc)
+    red(T.qm[:, 0:1], T.bt[:, 0:32], OP.max, kc)
+    kc = red(T.qm[:, 1:2], T.bt[:, 32:64], OP.max)
+    for q in range(N):
+        k = cp(T.g4[0:32, q:8:4], T.qm[quad(q), 0:2], kc)
+    red(T.tl[0:32, 0:1], T.g4[0:32, 0:4], OP.max, k)
+    k = red(T.tl[0:32, 1:2], T.g4[0:32, 4:8], OP.max)
+    for q in range(1, N):
+        kc = cp(T.tl[quad(q), :], T.tl[0:32, :], k)
+    k_dp = act(T.dp[:], T.emb[:], AF.Identity, T.tl[:, 0:1], -1.0, kc, k_eb)
+    k_i = ts(T.ini[:], T.tl[:, 1:2], DF + 0.5, DEL, OP.subtract, OP.mult, kc)
+    k_gd = ts(T.gd[:], T.em[:], T.tl[:, 0:1], DEL, OP.is_equal, OP.mult)
+    k = scan(T.nq[:], T.gd[:], T.zf[:], T.ini[:], k_gd, k_i)
+    k = tt(T.mk2[:], T.dp[:], T.nq[:], OP.is_gt, k, k_dp)
+    k_c2 = scan(T.cum2[:], T.mk2[:], T.zb[:], 0.0, k)
+    ka = acc(T.jkb[:, 640:960], T.cum2[:], AF.Sign, T.csn[:, 0:1], T.cnt2[:, 0:1], k_c2)
+    k = ts(T.jke[:, 0:320], T.cum2[:], T.csp[:, 1:2], 2.0, OP.is_gt, OP.mult, k_c2)
+    k = red(T.cnt2[:, 1:2], T.jke[:, 0:321], OP.add, k)
+    kc = ts(T.cnt2[:, 2:4], T.cnt2[:, 0:2], -2.0 * HB, None, OP.add, None, k, ka)
+    for i, b in enumerate(order):
+        for q in range(N):
+            ko = ts(T.off2[quad(q), 4 * i:4 * i + 4], T.cnt2[quad(b), 0:4], -0.5, NX / 2.0, OP.mult, OP.add, kc)
+        o = slice(64 * i, 64 * i + 64)
+        kk = pickq(T.sl2[:, o], T.xw[:], T.off2[:, 4 * i:4 * i + 4], ko, d_xw)
+        ks = picks(T.ss2[:, o], T.xws[:], T.off2[:, 4 * i:4 * i + 4], ko, d_xw)
+        d = slice(64 * rank, 64 * rank + 64)
+        send(b, c8(T.land2[:, d]), c8(T.sl2[:, o]), "arrb", kk)
+        send(b, T.lans2[:, d], T.ss2[:, o], "arrb", ks)
+    for i in range(3):
+        kw = op("a", lambda e: e.activation(T.wg[:, 32 * i:32 * i + 32], T.num[:].indirect(T.off2[:, 4 * i:4 * i + 2]), AF.Copy), k_n)
+    kw = op("v", lambda e: e.transpose(T.wtr[:], T.wg[:]), kw)
+    for i, b in enumerate(order):
+        send(b, T.lwho[:, rank:rank + 1], T.wtr[:, 32 * i:32 * i + 1], "aw", kw)
+
+    ab = ("arrb", arrivals(others, 2))
+    kf = pickq(T.fin[:], T.land2[:], T.ofin[:], ab, k_ofin, k_z2)
+    kfs = picks(T.fins[:], T.lans2[:], T.ofin[:], ab, k_ofin, k_z2s)
+    mm(bank(6, 128), T.vxq[:], T.vxs[:], T.fin[:, 0:128], T.fins[:, 0:128], True, False, kf, kfs, k_vx, k_vh)
+    ty = mm(bank(6, 128), T.vhq[:], T.vhs[:], T.fin[:, 128:256], T.fins[:, 128:256], False, True)
+    dma("s", "dout", T.oc[:], c8(T.fin[:, 128:256]), kf)
+    for k in range(2):
+        dma("s", "dout", T.osc[4 * k:4 * k + 4, :], T.fins[32 * k:32 * k + 4, 128:256], kfs)
+    for k in range(2, 4):
+        dma("a", "dout", T.osc[4 * k:4 * k + 4, :], T.fins[32 * k:32 * k + 4, 128:256], kfs)
+    ky = cp(T.ys[:], bank(6, 128), ty)
+    dma("a", "dout", T.y[:], T.ys[:], ky)
+    kw = op("v", lambda e: e.transpose(T.whot[:], T.lwho[:]), ("aw", arrivals(others, 1)), k_lw)
+    dma("s", "dout", T.who[:], T.whot[0:4, :], kw)
+    wait("g", [(s, n) for s, n in tot.items()])

@@ -3,15 +3,17 @@ from concourse.mybir import dt, AluOpType as OP, AxisListType, ActivationFunctio
 
 N, TOK, CAP, CB, DF = 4, 192, 80, 32, 80
 NX = N * CAP
+NH = NX // 2
 XC = 336
 HB = 352
-EPS, DEL, BIG, LOW = 1e-30, 1e-31, 1e29, -9e29
-RTB = [0, 1, 2, 3, 6, 7, 4, 5, 4, 7, 6, 5, 4]
-RTS = [7, 4, 9]
+EPS, BIG, LOW = 1e-30, 1e29, -9e29
+STEP = 2.0 ** -10
+RTB = [0, 1, 2, 3, 5, 4, 7, 6, 5, 4, 6, 7, 4, 5]
+RTS = [4, 6, 10]
 
 SCRATCH = {
     "rtt": ("sbuf", [128, 512], "bfloat16"), "rtq": ("sbuf", [128, 128], "float8_e4m3fn_x4"), "rts": ("sbuf", [128, 128], "uint8"),
-    "rpq": ("sbuf", [128, 416], "float8_e4m3fn_x4"), "rps": ("sbuf", [128, 416], "uint8"), "rto": ("sbuf", [128, 26], "uint16"),
+    "rpq": ("sbuf", [128, 448], "float8_e4m3fn_x4"), "rps": ("sbuf", [128, 448], "uint8"), "rto": ("sbuf", [128, 28], "uint16"),
     "xt": ("sbuf", [128, 776], "bfloat16"), "xq": ("sbuf", [128, 194], "float8_e4m3fn_x4"), "xs": ("sbuf", [128, 194], "uint8"),
     "wt": ("sbuf", [128, 2048], "bfloat16"), "wq": ("sbuf", [128, 512], "float8_e4m3fn_x4"), "wsc": ("sbuf", [128, 512], "uint8"),
     "r2t": ("sbuf", [128, 512], "bfloat16"), "r2q": ("sbuf", [128, 128], "float8_e4m3fn_x4"), "r2s": ("sbuf", [128, 128], "uint8"),
@@ -25,29 +27,28 @@ SCRATCH = {
     "xw": ("sbuf", [128, 704], "float8_e4m3fn_x4"), "xws": ("sbuf", [128, 704], "uint8"),
     "sl2": ("sbuf", [128, 192], "float8_e4m3fn_x4"), "ss2": ("sbuf", [128, 192], "uint8"),
     "land2": ("sbuf", [128, 256], "float8_e4m3fn_x4"), "lans2": ("sbuf", [128, 256], "uint8"),
-    "fin": ("sbuf", [128, 256], "float8_e4m3fn_x4"), "fins": ("sbuf", [128, 256], "uint8"),
+    "fin": ("sbuf", [128, 128], "float8_e4m3fn_x4"), "fins": ("sbuf", [128, 128], "uint8"),
     "lwho": ("sbuf", [128, 32], "float32"), "whot": ("sbuf", [128, 32], "float32"),
     "z1": ("sbuf", [128, 192], "float32"), "z2": ("sbuf", [128, 192], "float32"), "z3": ("sbuf", [128, 192], "float32"),
-    "mk": ("sbuf", [128, 192], "bfloat16"), "cum": ("sbuf", [128, 192], "bfloat16"), "zb": ("sbuf", [128, 320], "bfloat16"), "zf": ("sbuf", [128, 320], "float32"),
+    "mk": ("sbuf", [128, 192], "bfloat16"), "cum": ("sbuf", [128, 192], "bfloat16"), "zb": ("sbuf", [128, 320], "bfloat16"), "zf": ("sbuf", [128, 32], "float32"),
     "jka": ("sbuf", [128, 1152], "bfloat16"), "jkd": ("sbuf", [128, 512], "bfloat16"),
     "cnt1": ("sbuf", [128, 8], "float32"), "cntm": ("sbuf", [128, 4], "float32"), "off1": ("sbuf", [128, 24], "uint16"), "ozero": ("sbuf", [128, 4], "uint16"),
     "inv": ("sbuf", [128, 320], "float32"), "em": ("sbuf", [128, 320], "float32"), "emb": ("sbuf", [128, 320], "float32"),
-    "y1": ("sbuf", [128, 320], "float32"), "y2": ("sbuf", [128, 320], "float32"), "ns": ("sbuf", [128, 320], "float32"),
-    "gd": ("sbuf", [128, 320], "float32"), "nq": ("sbuf", [128, 320], "float32"), "dp": ("sbuf", [128, 320], "float32"),
+    "y1": ("sbuf", [128, 320], "float32"), "y2": ("sbuf", [128, 320], "float32"), "sn": ("sbuf", [128, 320], "float32"), "ns": ("sbuf", [128, 320], "float32"),
+    "gd": ("sbuf", [128, 320], "bfloat16"), "nq": ("sbuf", [128, 320], "bfloat16"), "sg": ("sbuf", [128, 320], "bfloat16"), "cap": ("sbuf", [128, 320], "bfloat16"),
     "mk2": ("sbuf", [128, 320], "bfloat16"), "cum2": ("sbuf", [128, 320], "bfloat16"),
     "jk2": ("sbuf", [128, 960], "bfloat16"), "jkb": ("sbuf", [128, 960], "bfloat16"), "jke": ("sbuf", [128, 336], "bfloat16"),
     "en": ("sbuf", [128, 4], "float32"), "lt": ("sbuf", [128, 4], "float32"), "pen": ("sbuf", [128, 4], "float32"),
-    "c1": ("sbuf", [128, 4], "float32"), "c2": ("sbuf", [128, 4], "float32"), "cc": ("sbuf", [128, 2], "float32"),
-    "bc": ("sbuf", [128, 64], "float32"), "bt": ("sbuf", [128, 64], "float32"), "qm": ("sbuf", [128, 2], "float32"),
-    "g4": ("sbuf", [128, 8], "float32"), "tl": ("sbuf", [128, 2], "float32"), "ini": ("sbuf", [128, 1], "float32"),
+    "bc": ("sbuf", [128, 192], "float32"), "bt": ("sbuf", [128, 192], "float32"), "qm": ("sbuf", [128, 2], "float32"),
+    "g4": ("sbuf", [128, 2], "float32"), "tl": ("sbuf", [128, 2], "float32"), "ini": ("sbuf", [128, 1], "float32"),
     "cnt2": ("sbuf", [128, 4], "float32"), "off2": ("sbuf", [128, 12], "uint16"),
     "nb": ("sbuf", [128, 320], "bfloat16"), "num": ("sbuf", [128, XC], "float32"), "wg": ("sbuf", [128, 96], "float32"), "wtr": ("sbuf", [128, 96], "float32"),
     "ys": ("sbuf", [128, 128], "float32"),
     "th1": ("sbuf", [128, 1], "float32"), "eb1": ("sbuf", [128, 1], "float32"), "th2": ("sbuf", [128, 1], "float32"), "eb2": ("sbuf", [128, 1], "float32"),
     "pI": ("sbuf", [128, 16], "int32"), "rI": ("sbuf", [128, 16], "int32"), "qI": ("sbuf", [128, 16], "int32"),
-    "b16": ("sbuf", [128, 8], "int32"), "b32": ("sbuf", [128, 8], "int32"), "bfin": ("sbuf", [128, 16], "int32"), "ofi": ("sbuf", [128, 16], "int32"),
+    "b16": ("sbuf", [128, 8], "int32"), "b32": ("sbuf", [128, 8], "int32"), "bfin": ("sbuf", [128, 8], "int32"), "ofi": ("sbuf", [128, 8], "int32"),
     "cs": ("sbuf", [128, 8], "float32"), "csp": ("sbuf", [128, 8], "float32"), "csn": ("sbuf", [128, 8], "float32"), "cm": ("sbuf", [128, 8], "float32"), "cmn": ("sbuf", [128, 8], "float32"),
-    "i80": ("sbuf", [128, 80], "float32"), "ofin": ("sbuf", [128, 16], "uint16"),
+    "i80": ("sbuf", [128, 80], "float32"), "ofin": ("sbuf", [128, 8], "uint16"),
     "ps": ("psum", [128, 4096], "float32"),
 }
 SEMAPHORES = ["v", "a", "t", "gq", "dx", "drt", "dw", "dr2", "dvx", "dvh", "dxw", "dnb", "dout", "ls",
@@ -102,7 +103,7 @@ def rank_program(g, core, T, topo):
     tt = lambda out, x, y, o, *d: op("v", lambda e: e.tensor_tensor(out, x, y, o), *d)
     cp = lambda out, x, *d: op("v", lambda e: e.tensor_copy(out, x), *d)
     red = lambda out, x, o, *d: op("v", lambda e: e.tensor_reduce(out, x, AxisListType.X, o), *d)
-    scan = lambda out, x, y, i, *d: op("v", lambda e: e.tensor_tensor_scan(out, x, y, i, OP.add, OP.add), *d)
+    scan = lambda out, x, y, i, o, *d: op("v", lambda e: e.tensor_tensor_scan(out, x, y, i, OP.add, o), *d)
     quant = lambda q, s, x, *d: op("v", lambda e: e.quantize_mx(q, s, x), *d)
     act = lambda out, x, f, b, s, *d: op("a", lambda e: e.activation(out, x, f, bias=b, scale=s), *d)
     acc = lambda out, x, f, b, o, *d: op("a", lambda e: e.activation(out, x, f, bias=b, scale=1.0, accum_out=o), *d)
@@ -125,13 +126,11 @@ def rank_program(g, core, T, topo):
     gi(T.pI[:], [[0, 16]], 1)
     gi(T.b16[:], [[16, 8]], 0)
     k_g = gi(T.b32[:], [[32, 8]], 0)
-    k_fin = gi(T.bfin[:], [[32, 2], [64, 4], [16, 2]], 0)
+    k_fin = gi(T.bfin[:], [[64, 4], [16, 2]], 0)
     k_80 = op("g", lambda e: e.iota(T.i80[:], [[1, 80]], 0, 0, allow_small_or_imprecise_dtypes=True))
     ms(T.rtt[:, 32:512], 0.0)
-    c = 0
-    while c < 13:
+    for c in range(len(RTB)):
         k_rto = ms(T.rto[:, 2 * c:2 * c + 2], RTB[c])
-        c += 1
     k_x0 = ms(T.xt[:, 768:776], 0.0)
     ms(T.th1[0:64, :], -EPS / 2)
     ms(T.th1[64:128, :], EPS / 2)
@@ -153,23 +152,24 @@ def rank_program(g, core, T, topo):
 
     k = ts(T.rtt[:, 16:32], T.rtt[:, 0:16], -1.0, None, OP.mult, None, d_rt)
     k_rq = quant(T.rtq[:], T.rts[:], T.rtt[:], k)
-    k_rp = pickq(T.rpq[:], T.rtq[:], T.rto[:], k_rq)
-    k_rs = picks(T.rps[:], T.rts[:], T.rto[:], k_rq, k_rto)
+    kp1 = pickq(T.rpq[:, 0:256], T.rtq[:], T.rto[:, 0:16], k_rq)
+    ks1 = picks(T.rps[:, 0:256], T.rts[:], T.rto[:, 0:16], k_rq, k_rto)
     k_xq = quant(T.xq[:], T.xs[:], T.xt[:], d_x, k_x0)
+    kp2 = pickq(T.rpq[:, 256:448], T.rtq[:], T.rto[:, 16:28])
+    ks2 = picks(T.rps[:, 256:448], T.rts[:], T.rto[:, 16:28])
     dm = []
     for j in range(3):
-        mm(bank(j, 192), T.rpq[:, 0:128], T.rps[:, 0:128], T.xq[:, 0:192], T.xs[:, 0:192], True, False, k_rp, k_rs, k_xq)
+        mm(bank(j, 192), T.rpq[:, 0:128], T.rps[:, 0:128], T.xq[:, 0:192], T.xs[:, 0:192], True, False, kp1, ks1, k_xq)
         a = 32 * RTS[j]
-        dm.append(mm(bank(j, 192), T.rpq[:, a:a + 128], T.rps[:, a:a + 128], T.xq[:, 0:192], T.xs[:, 0:192], False, True))
+        dj = (kp2, ks2) if j else ()
+        dm.append(mm(bank(j, 192), T.rpq[:, a:a + 128], T.rps[:, a:a + 128], T.xq[:, 0:192], T.xs[:, 0:192], False, True, *dj))
     k_z1 = act(T.z1[:], bank(0, 192), AF.Identity, T.eb1[:], 1.0, dm[0], k_th)
-    ms(T.jke[:, 320:321], -320.0)
-    ms(T.ozero[:], TOK)
     k2 = tt(T.cm[:], T.qI[:, 0:8], T.b32[:], OP.add, kq)
     k_cm = ts(T.cmn[:], T.cm[:], -1.0, -0.5, OP.mult, OP.add, k2)
     k = tt(T.z2[:], bank(1, 192), T.z1[:], OP.min, dm[1], k_z1)
     k_d1 = tt(T.z3[:], bank(2, 192), T.z2[:], OP.min, dm[2], k)
     k = ts(T.mk[:], T.z3[:], T.th1[:], None, OP.is_gt, None, k_d1)
-    k_cum = scan(T.cum[:], T.mk[:], T.zb[:, 0:192], 0.0, k)
+    k_cum = scan(T.cum[:], T.mk[:], T.zb[:, 0:192], 0.0, OP.add, k)
     k_a = [acc(T.jka[:, 192 * c:192 * c + 192], T.cum[:], AF.Sign, T.csn[:, c:c + 1], T.cnt1[:, c:c + 1], k_cum, k_cs) for c in range(3)]
     k3 = ts(T.jkd[:, 0:192], T.cum[:], T.csp[:, 3:4], 2.0, OP.is_gt, OP.mult, k_cum)
     k4 = ts(T.jkd[:, 256:448], T.cum[:], T.csp[:, 4:5], 2.0, OP.is_gt, OP.mult)
@@ -197,7 +197,8 @@ def rank_program(g, core, T, topo):
         if b != rank:
             send(b, T.msgi[:, 8 * rank:8 * rank + 2], T.msgo[:, o:o + 2], "am", m_v[b], m_a[b])
 
-    k_z = pickq(T.land1[:, NX:XC], T.xq[:, 0:194], T.ozero[:, 0:1], k_xq)
+    k_oz = ms(T.ozero[:], TOK)
+    k_z = pickq(T.land1[:, NX:XC], T.xq[:, 0:194], T.ozero[:, 0:1], k_xq, k_oz)
     k_zs = picks(T.lans1[:, NX:XC], T.xs[:, 0:194], T.ozero[:, 0:1], k_z)
     k_wq = quant(T.wq[:], T.wsc[:], T.wt[:], d_w)
     ms(T.r2t[:, 40:512], 0.0)
@@ -216,25 +217,30 @@ def rank_program(g, core, T, topo):
     k_vx = quant(T.vxq[:], T.vxs[:], T.vxt[:], d_vx)
     k_vh = quant(T.vhq[:], T.vhs[:], T.vht[:], d_vh)
     for q in range(N):
-        ms(T.th2[quad(q), :], EPS / 2 if q == srt[2] else -EPS / 2)
+        ms(T.th2[quad(q), :], -EPS / 2 if q == srt[2] else EPS / 2)
         k_t2 = ms(T.eb2[quad(q), :], -EPS if q == srt[1] else 0.0)
     ms(T.zf[:], 0.0)
+    ms(T.cap[:], 64 * STEP)
+    k_je = ms(T.jke[:, 320:321], -320.0)
     k_num = ms(T.num[:], -1.0)
-    k = tt(T.ofi[:], T.rI[:], T.bfin[:], OP.add, k_fin)
+    k = ts(T.ofi[:], T.bfin[:], 32.0, None, OP.add, None, k_fin)
+    k = tt(T.ofi[:], T.rI[:, 0:8], T.ofi[:], OP.add, k)
     k_ofin = cp(T.ofin[:], T.ofi[:], k)
 
     arr = lambda s: ("arr%d" % s, arrivals([s], 2))
     home = (pk[rank], psc[rank])
-    halves = [(0, 160, [0, 1]), (160, NX + 2, [2, 3])]
-    kq_h = []
+    halves = [(0, NH, [0, 1]), (NH, NX + 2, [2, 3])]
+    W = []
     for h, (c0, c1, who) in enumerate(halves):
         deps = [arr(s) for s in who if s != rank] + list(home) + [k_z, k_zs, k_wq, k_d1, k_z1]
-        w = [mm(bank(4 * h + i, c1 - c0), T.wq[:, 128 * i:128 * i + 128], T.wsc[:, 128 * i:128 * i + 128], T.land1[:, c0:c1], T.lans1[:, c0:c1], True, True, *deps) for i in range(4)]
+        W.append([mm(bank(4 * h + i, c1 - c0), T.wq[:, 128 * i:128 * i + 128], T.wsc[:, 128 * i:128 * i + 128], T.land1[:, c0:c1], T.lans1[:, c0:c1], True, True, *deps) for i in range(4)])
+    kq_h = []
+    for h, (c0, c1, who) in enumerate(halves):
         hv = lambda i: T.hb[:, 4 * c0 + i:4 * c1:4]
-        k0 = act(hv(0), bank(4 * h, c1 - c0), AF.Relu, 0.0, 0.0625, w[0])
-        k1 = ts(hv(1), bank(4 * h + 1, c1 - c0), 0.0, 0.0625, OP.max, OP.mult, w[1])
-        k2 = act(hv(2), bank(4 * h + 2, c1 - c0), AF.Relu, 0.0, 0.0625, w[2])
-        k3 = ts(hv(3), bank(4 * h + 3, c1 - c0), 0.0, 0.0625, OP.max, OP.mult, w[3])
+        k0 = act(hv(0), bank(4 * h, c1 - c0), AF.Relu, 0.0, 0.0625, W[h][0])
+        k1 = ts(hv(1), bank(4 * h + 1, c1 - c0), 0.0, 0.0625, OP.max, OP.mult, W[h][1])
+        k2 = act(hv(2), bank(4 * h + 2, c1 - c0), AF.Relu, 0.0, 0.0625, W[h][2])
+        k3 = ts(hv(3), bank(4 * h + 3, c1 - c0), 0.0, 0.0625, OP.max, OP.mult, W[h][3])
         kq_h.append(quant(T.xw[:, HB + c0:HB + c1], T.xws[:, HB + c0:HB + c1], T.hb[:, 4 * c0:4 * c1], k0, k1, k2, k3))
     alla = [arr(s) for s in range(N) if s != rank]
     dma("s", "dxw", c8(T.xw[:, 0:XC]), c8(T.land1[:]), *alla, *home, k_z, k_zs)
@@ -245,53 +251,56 @@ def rank_program(g, core, T, topo):
 
     H = lambda a, b: (T.xw[:, HB + a:HB + b], T.xws[:, HB + a:HB + b])
     P = lambda k: (T.r2p[:, 128 * k:128 * k + 128], T.r2ps[:, 128 * k:128 * k + 128])
-    e0 = mm(bank(1, 128), *H(0, 128), T.r2q[:], T.r2s[:], True, True, kq_h[0], k_r2p, k_r2s, k_r2q)
-    t_e = mm(bank(0, NX), *P(3), *H(0, NX), True, True, kq_h[1])
-    e1 = mm(bank(2, 128), *H(128, 256), T.r2q[:], T.r2s[:], True, True)
-    e2 = mm(bank(3, 128), *H(192, 320), T.r2q[:], T.r2s[:], True, True)
-    mm(bank(4, NX), *P(0), *H(0, NX), True, False)
-    f1 = mm(bank(4, NX), *P(1), *H(0, NX), False, True)
-    mm(bank(5, NX), *P(0), *H(0, NX), True, False)
-    f2 = mm(bank(5, NX), *P(2), *H(0, NX), False, True)
-    ken = [act(T.en[:, k:k + 1], T.ps[:, 512 * (k + 1) + 4:512 * (k + 1) + 5], AF.Copy, 0.0, 1.0, e) for k, e in enumerate((e0, e1, e2))]
+    ea = mm(bank(0, NH), *P(3), *H(0, NH), True, True, kq_h[0], k_r2p, k_r2s, k_r2q)
+    e0 = mm(bank(1, 128), *H(0, 128), T.r2q[:], T.r2s[:], True, True)
+    mm(bank(2, NH), *P(0), *H(0, NH), True, False)
+    fa = mm(bank(2, NH), *P(1), *H(0, NH), False, True)
+    eb = mm(bank(4, NH), *P(3), *H(NH, NX), True, True, kq_h[1])
+    e1 = mm(bank(5, 128), *H(128, 256), T.r2q[:], T.r2s[:], True, True)
+    e2 = mm(bank(6, 128), *H(192, 320), T.r2q[:], T.r2s[:], True, True)
+    mm(bank(7, NH), *P(0), *H(NH, NX), True, False)
+    fb = mm(bank(7, NH), *P(1), *H(NH, NX), False, True)
+    mm(bank(3, NX), *P(0), *H(0, NX), True, False)
+    f2 = mm(bank(3, NX), *P(2), *H(0, NX), False, True)
+    e4 = lambda k: T.ps[:, 512 * k + 4:512 * k + 5]
+    ken0 = act(T.en[:, 0:1], e4(1), AF.Copy, 0.0, 1.0, e0)
+    act(T.y1[:, 0:NH], bank(2, NH), AF.Identity, T.eb2[:], 1.0, fa, k_t2)
+    ken1 = act(T.en[:, 1:2], e4(5), AF.Copy, 0.0, 1.0, e1)
+    ken2 = act(T.en[:, 2:3], e4(6), AF.Copy, 0.0, 1.0, e2)
+    k_y1 = act(T.y1[:, NH:NX], bank(7, NH), AF.Identity, T.eb2[:], 1.0, fb)
     for s in range(N):
         ki = ts(T.inv[:, 80 * s:80 * s + 80], T.i80[:], T.msgi[:, 8 * s + 1:8 * s + 2], BIG, OP.is_ge, OP.mult, k_80, am, m_v[rank])
-    k_em = tt(T.em[:], bank(0, NX), T.inv[:], OP.add, t_e, ki)
-    kl = []
-    for k in range(3):
-        kc = ts(T.jk2[:, 320 * k:320 * k + 320], T.em[:], T.en[:, k:k + 1], None, OP.is_lt, None, k_em, ken[k])
-        if k < 2:
-            kl.append(acc(T.jkb[:, 320 * k:320 * k + 320], T.jk2[:, 320 * k:320 * k + 320], AF.Copy, 0.0, T.lt[:, k:k + 1], kc))
-        else:
-            kl.append(red(T.lt[:, k:k + 1], T.jk2[:, 320 * k:320 * k + 320], OP.add, kc))
-    k_y1 = act(T.y1[:], bank(4, NX), AF.Identity, T.eb2[:], 1.0, f1, k_t2)
+    tt(T.em[:, 0:NH], bank(0, NH), T.inv[:, 0:NH], OP.add, ea, ki)
+    k_em = tt(T.em[:, NH:NX], bank(4, NH), T.inv[:, NH:NX], OP.add, eb)
+    kc0 = ts(T.jk2[:, 0:320], T.em[:], T.en[:, 0:1], None, OP.is_lt, None, k_em, ken0)
+    kc1 = ts(T.jk2[:, 320:640], T.em[:], T.en[:, 1:2], None, OP.is_lt, None, ken1)
+    k = act(T.jk2[:, 640:960], T.em[:], AF.Sign, T.en[:, 2:3], -1.0, k_em, ken2)
+    kl0 = acc(T.jkb[:, 0:320], T.jk2[:, 0:320], AF.Copy, 0.0, T.lt[:, 0:1], kc0)
+    kl2 = acc(T.jkb[:, 320:640], T.jk2[:, 640:960], AF.Relu, 0.0, T.lt[:, 2:3], k)
+    kl1 = red(T.lt[:, 1:2], T.jk2[:, 320:640], OP.add, kc1)
+    k_y2 = tt(T.y2[:], bank(3, NX), T.y1[:], OP.min, f2, k_y1)
+    k = act(T.sn[:], T.y2[:], AF.Sign, T.th2[:], 1.0, k_y2)
+    k_ns = act(T.ns[:], T.sn[:], AF.Relu, 0.0, -BIG, k)
     for s in range(N):
         k_n = act(T.num[0:1, 80 * s:80 * s + 80], T.nb[0:1, 80 * s:80 * s + 80], AF.Copy, float(TOK * s), 1.0, d_nb, k_num)
-    kp = ts(T.pen[:, 0:3], T.lt[:, 0:3], DF - 0.5, LOW, OP.is_ge, OP.mult, *kl)
-    k_y2 = tt(T.y2[:], bank(5, NX), T.y1[:], OP.min, f2, k_y1)
-    tt(T.c1[:, 0:3], T.en[:, 0:3], T.pen[:, 0:3], OP.add, kp)
-    kc = tt(T.c2[:, 0:3], T.lt[:, 0:3], T.pen[:, 0:3], OP.add)
-    k_ns = ts(T.ns[:], T.y2[:], T.th2[:], BIG, OP.is_le, OP.mult, k_y2)
-    red(T.cc[:, 0:1], T.c1[:, 0:3], OP.max, kc)
-    kc = red(T.cc[:, 1:2], T.c2[:, 0:3], OP.max)
-    k_eb = tt(T.emb[:], T.em[:], T.ns[:], OP.add, k_ns)
-    ts(T.bc[:, 0:32], T.zf[:, 0:32], T.cc[:, 0:1], None, OP.add, None, kc)
-    kc = ts(T.bc[:, 32:64], T.zf[:, 0:32], T.cc[:, 1:2], None, OP.add, None)
+    kp = ts(T.pen[:, 0:3], T.lt[:, 0:3], DF - 0.5, LOW, OP.is_ge, OP.mult, kl0, kl1, kl2)
+    for k in range(3):
+        ts(T.bc[:, 32 * k:32 * k + 32], T.zf[:], T.en[:, k:k + 1], T.pen[:, k:k + 1], OP.add, OP.add, kp)
+        kc = ts(T.bc[:, 96 + 32 * k:128 + 32 * k], T.zf[:], T.lt[:, k:k + 1], T.pen[:, k:k + 1], OP.add, OP.add)
     kc = op("v", lambda e: e.transpose(T.bt[:], T.bc[:]), kc)
-    red(T.qm[:, 0:1], T.bt[:, 0:32], OP.max, kc)
-    kc = red(T.qm[:, 1:2], T.bt[:, 32:64], OP.max)
+    k_eb = tt(T.emb[:], T.em[:], T.ns[:], OP.add, k_ns)
+    red(T.qm[:, 0:1], T.bt[:, 0:96], OP.max, kc)
+    kc = red(T.qm[:, 1:2], T.bt[:, 96:192], OP.max)
+    tt(T.g4[0:64, :], T.qm[0:64, :], T.qm[64:128, :], OP.max, kc)
+    kc = tt(T.g4[64:128, :], T.qm[64:128, :], T.qm[0:64, :], OP.max)
     for q in range(N):
-        k = cp(T.g4[0:32, q:8:4], T.qm[quad(q), 0:2], kc)
-    red(T.tl[0:32, 0:1], T.g4[0:32, 0:4], OP.max, k)
-    k = red(T.tl[0:32, 1:2], T.g4[0:32, 4:8], OP.max)
-    for q in range(1, N):
-        kc = cp(T.tl[quad(q), :], T.tl[0:32, :], k)
-    k_dp = act(T.dp[:], T.emb[:], AF.Identity, T.tl[:, 0:1], -1.0, kc, k_eb)
-    k_i = ts(T.ini[:], T.tl[:, 1:2], DF + 0.5, DEL, OP.subtract, OP.mult, kc)
-    k_gd = ts(T.gd[:], T.em[:], T.tl[:, 0:1], DEL, OP.is_equal, OP.mult)
-    k = scan(T.nq[:], T.gd[:], T.zf[:], T.ini[:], k_gd, k_i)
-    k = tt(T.mk2[:], T.dp[:], T.nq[:], OP.is_gt, k, k_dp)
-    k_c2 = scan(T.cum2[:], T.mk2[:], T.zb[:], 0.0, k)
+        k = tt(T.tl[quad(q), :], T.g4[quad(q), :], T.g4[quad(q ^ 1), :], OP.max, kc)
+    k_sg = act(T.sg[:], T.emb[:], AF.Sign, T.tl[:, 0:1], -1.0, k, k_eb)
+    k_gd = ts(T.gd[:], T.em[:], T.tl[:, 0:1], STEP, OP.is_equal, OP.mult, k)
+    k_i = ts(T.ini[:], T.tl[:, 1:2], DF + 0.5, STEP, OP.subtract, OP.mult)
+    k = scan(T.nq[:], T.gd[:], T.cap[:], T.ini[:], OP.min, k_i)
+    k = tt(T.mk2[:], T.sg[:], T.nq[:], OP.is_gt, k, k_sg)
+    k_c2 = scan(T.cum2[:], T.mk2[:], T.zb[:], 0.0, OP.add, k)
     ka = acc(T.jkb[:, 640:960], T.cum2[:], AF.Sign, T.csn[:, 0:1], T.cnt2[:, 0:1], k_c2)
     k = ts(T.jke[:, 0:320], T.cum2[:], T.csp[:, 1:2], 2.0, OP.is_gt, OP.mult, k_c2)
     k = red(T.cnt2[:, 1:2], T.jke[:, 0:321], OP.add, k)
@@ -312,16 +321,15 @@ def rank_program(g, core, T, topo):
         send(b, T.lwho[:, rank:rank + 1], T.wtr[:, 32 * i:32 * i + 1], "aw", kw)
 
     ab = ("arrb", arrivals(others, 2))
-    kf = pickq(T.fin[:], T.land2[:], T.ofin[:], ab, k_ofin, k_z2)
-    kfs = picks(T.fins[:], T.lans2[:], T.ofin[:], ab, k_ofin, k_z2s)
-    mm(bank(6, 128), T.vxq[:], T.vxs[:], T.fin[:, 0:128], T.fins[:, 0:128], True, False, kf, kfs, k_vx, k_vh)
-    ty = mm(bank(6, 128), T.vhq[:], T.vhs[:], T.fin[:, 128:256], T.fins[:, 128:256], False, True)
-    dma("s", "dout", T.oc[:], c8(T.fin[:, 128:256]), kf)
-    for k in range(2):
-        dma("s", "dout", T.osc[4 * k:4 * k + 4, :], T.fins[32 * k:32 * k + 4, 128:256], kfs)
-    for k in range(2, 4):
-        dma("a", "dout", T.osc[4 * k:4 * k + 4, :], T.fins[32 * k:32 * k + 4, 128:256], kfs)
-    ky = cp(T.ys[:], bank(6, 128), ty)
+    mm(bank(5, 224), T.vxq[:], T.vxs[:], T.land2[:, 0:224], T.lans2[:, 0:224], True, False, ab, k_z2, k_z2s, k_vx, k_vh, ken1)
+    ty = mm(bank(5, 224), T.vhq[:], T.vhs[:], T.land2[:, 32:256], T.lans2[:, 32:256], False, True)
+    kf = pickq(T.fin[:], T.land2[:], T.ofin[:], ab, k_ofin)
+    kfs = picks(T.fins[:], T.lans2[:], T.ofin[:], ab, k_ofin)
+    for a in range(N):
+        ky = cp(T.ys[:, CB * a:CB * a + CB], T.ps[:, 2560 + 64 * a:2560 + 64 * a + CB], ty)
+    dma("s", "dout", T.oc[:], c8(T.fin[:]), kf)
+    for k in range(4):
+        dma("s" if k < 2 else "a", "dout", T.osc[4 * k:4 * k + 4, :], T.fins[32 * k:32 * k + 4, :], kfs)
     dma("a", "dout", T.y[:], T.ys[:], ky)
     kw = op("v", lambda e: e.transpose(T.whot[:], T.lwho[:]), ("aw", arrivals(others, 1)), k_lw)
     dma("s", "dout", T.who[:], T.whot[0:4, :], kw)

from concourse.bass import DstId, RemoteDMATransfer
from concourse.mybir import dt, AluOpType as OP, AxisListType, ActivationFunctionType as AF

N, TOK, CAP, CB, DF = 4, 192, 80, 32, 80
NX = N * CAP
NH = NX // 2
XC = 336
HB = 352
EPS, BIG, LOW = 1e-30, 1e29, -9e29
STEP = 2.0 ** -10
RTB = [0, 1, 2, 3, 5, 4, 7, 6, 5, 4, 6, 7, 4, 5]
RTS = [4, 6, 10]

SCRATCH = {
    "rtt": ("sbuf", [128, 512], "bfloat16"), "rtq": ("sbuf", [128, 128], "float8_e4m3fn_x4"), "rts": ("sbuf", [128, 128], "uint8"),
    "rpq": ("sbuf", [128, 448], "float8_e4m3fn_x4"), "rps": ("sbuf", [128, 448], "uint8"), "rto": ("sbuf", [128, 28], "uint16"),
    "xt": ("sbuf", [128, 776], "bfloat16"), "xq": ("sbuf", [128, 194], "float8_e4m3fn_x4"), "xs": ("sbuf", [128, 194], "uint8"),
    "wt": ("sbuf", [128, 2048], "bfloat16"), "wq": ("sbuf", [128, 512], "float8_e4m3fn_x4"), "wsc": ("sbuf", [128, 512], "uint8"),
    "r2t": ("sbuf", [128, 512], "bfloat16"), "r2q": ("sbuf", [128, 128], "float8_e4m3fn_x4"), "r2s": ("sbuf", [128, 128], "uint8"),
    "r2p": ("sbuf", [128, 512], "float8_e4m3fn_x4"), "r2ps": ("sbuf", [128, 512], "uint8"), "r2o": ("sbuf", [128, 32], "uint16"),
    "vxt": ("sbuf", [128, 512], "bfloat16"), "vxq": ("sbuf", [128, 128], "float8_e4m3fn_x4"), "vxs": ("sbuf", [128, 128], "uint8"),
    "vht": ("sbuf", [128, 512], "bfloat16"), "vhq": ("sbuf", [128, 128], "float8_e4m3fn_x4"), "vhs": ("sbuf", [128, 128], "uint8"),
    "hb": ("sbuf", [128, 4 * (NX + 2)], "bfloat16"),
    "sl1": ("sbuf", [128, 240], "float8_e4m3fn_x4"), "ss1": ("sbuf", [128, 240], "uint8"),
    "land1": ("sbuf", [128, XC], "float8_e4m3fn_x4"), "lans1": ("sbuf", [128, XC], "uint8"),
    "msgo": ("sbuf", [128, 32], "bfloat16"), "msgi": ("sbuf", [128, 32], "bfloat16"),
    "xw": ("sbuf", [128, 704], "float8_e4m3fn_x4"), "xws": ("sbuf", [128, 704], "uint8"),
    "sl2": ("sbuf", [128, 192], "float8_e4m3fn_x4"), "ss2": ("sbuf", [128, 192], "uint8"),
    "land2": ("sbuf", [128, 256], "float8_e4m3fn_x4"), "lans2": ("sbuf", [128, 256], "uint8"),
    "fin": ("sbuf", [128, 128], "float8_e4m3fn_x4"), "fins": ("sbuf", [128, 128], "uint8"),
    "lwho": ("sbuf", [128, 32], "float32"), "whot": ("sbuf", [128, 32], "float32"),
    "z1": ("sbuf", [128, 192], "float32"), "z2": ("sbuf", [128, 192], "float32"), "z3": ("sbuf", [128, 192], "float32"),
    "mk": ("sbuf", [128, 192], "bfloat16"), "cum": ("sbuf", [128, 192], "bfloat16"), "zb": ("sbuf", [128, 320], "bfloat16"), "zf": ("sbuf", [128, 32], "float32"),
    "jka": ("sbuf", [128, 1152], "bfloat16"), "jkd": ("sbuf", [128, 512], "bfloat16"),
    "cnt1": ("sbuf", [128, 8], "float32"), "cntm": ("sbuf", [128, 4], "float32"), "off1": ("sbuf", [128, 24], "uint16"), "ozero": ("sbuf", [128, 4], "uint16"),
    "inv": ("sbuf", [128, 320], "float32"), "em": ("sbuf", [128, 320], "float32"), "emb": ("sbuf", [128, 320], "float32"),
    "y1": ("sbuf", [128, 320], "float32"), "y2": ("sbuf", [128, 320], "float32"), "sn": ("sbuf", [128, 320], "float32"), "ns": ("sbuf", [128, 320], "float32"),
    "gd": ("sbuf", [128, 320], "bfloat16"), "nq": ("sbuf", [128, 320], "bfloat16"), "sg": ("sbuf", [128, 320], "bfloat16"), "cap": ("sbuf", [128, 320], "bfloat16"),
    "mk2": ("sbuf", [128, 320], "bfloat16"), "cum2": ("sbuf", [128, 320], "bfloat16"),
    "jk2": ("sbuf", [128, 960], "bfloat16"), "jkb": ("sbuf", [128, 960], "bfloat16"), "jke": ("sbuf", [128, 336], "bfloat16"),
    "en": ("sbuf", [128, 4], "float32"), "lt": ("sbuf", [128, 4], "float32"), "pen": ("sbuf", [128, 4], "float32"),
    "bc": ("sbuf", [128, 192], "float32"), "bt": ("sbuf", [128, 192], "float32"), "qm": ("sbuf", [128, 2], "float32"),
    "g4": ("sbuf", [128, 2], "float32"), "tl": ("sbuf", [128, 2], "float32"), "ini": ("sbuf", [128, 1], "float32"),
    "cnt2": ("sbuf", [128, 4], "float32"), "off2": ("sbuf", [128, 12], "uint16"),
    "nb": ("sbuf", [128, 320], "bfloat16"), "num": ("sbuf", [128, XC], "float32"), "wg": ("sbuf", [128, 96], "float32"), "wtr": ("sbuf", [128, 96], "float32"),
    "ys": ("sbuf", [128, 128], "float32"),
    "th1": ("sbuf", [128, 1], "float32"), "eb1": ("sbuf", [128, 1], "float32"), "th2": ("sbuf", [128, 1], "float32"), "eb2": ("sbuf", [128, 1], "float32"),
    "pI": ("sbuf", [128, 16], "int32"), "rI": ("sbuf", [128, 16], "int32"), "qI": ("sbuf", [128, 16], "int32"),
    "b16": ("sbuf", [128, 8], "int32"), "b32": ("sbuf", [128, 8], "int32"), "bfin": ("sbuf", [128, 8], "int32"), "ofi": ("sbuf", [128, 8], "int32"),
    "cs": ("sbuf", [128, 8], "float32"), "csp": ("sbuf", [128, 8], "float32"), "csn": ("sbuf", [128, 8], "float32"), "cm": ("sbuf", [128, 8], "float32"), "cmn": ("sbuf", [128, 8], "float32"),
    "i80": ("sbuf", [128, 80], "float32"), "ofin": ("sbuf", [128, 8], "uint16"),
    "ps": ("psum", [128, 4096], "float32"),
}
SEMAPHORES = ["v", "a", "t", "gq", "dx", "drt", "dw", "dr2", "dvx", "dvh", "dxw", "dnb", "dout", "ls",
              "arr0", "arr1", "arr2", "arr3", "am", "arrb", "aw"]


def rank_program(g, core, T, topo):
    rank = T.rank_of(core)
    if rank is None:
        return
    cores = list(T.cores)
    me_chip = topo.chip(core)
    others = [(rank + 1 + k) % N for k in range(N - 1)]
    order = [b for b in others if not topo.same_plane(topo.chip(cores[b]), me_chip)] + \
            [b for b in others if topo.same_plane(topo.chip(cores[b]), me_chip)]
    eng = {"v": g.vector, "a": g.scalar, "t": g.tensor, "s": g.sync, "g": g}
    semof = {"v": "v", "a": "a", "t": "t", "g": "gq"}
    tot, seen = {}, {q: {} for q in eng}

    def wait(q, deps):
        for s, n in deps:
            if seen[q].get(s, 0) < n:
                eng[q].wait_ge(T.sem[s], n)
                seen[q][s] = n

    def op(q, fn, *deps):
        wait(q, deps)
        s = semof[q]
        fn(eng[q]).then_inc(T.sem[s], 1)
        tot[s] = tot.get(s, 0) + 1
        return (s, tot[s])

    def dma(q, s, out, src, *deps):
        wait(q, deps)
        eng[q].dma_start(out, src).then_inc(T.sem[s], 16)
        tot[s] = tot.get(s, 0) + 16
        return (s, tot[s])

    def send(b, out, src, sem, *deps):
        wait("g", deps)
        rid, pid, _ = topo.addr(cores[b])
        g.remote_dma(out, src, T.sem[sem], T.sem.ls, pid, rid, topo.mask(core, cores[b]))
        tot["ls"] = tot.get("ls", 0) + len(topo.engines(core, cores[b]))

    def arrivals(srcs, per):
        return per * sum(len(topo.engines(cores[s], core)) for s in srcs)

    u8, u32 = dt.uint8, dt.uint32
    c8 = lambda v: v.bitcast(u8)
    ms = lambda ap, val, *d: op("v", lambda e: e.memset(ap, val), *d)
    ts = lambda out, x, s1, s2, o0, o1, *d: op("v", lambda e: e.tensor_scalar(out, x, s1, s2, o0) if o1 is None else e.tensor_scalar(out, x, s1, s2, o0, o1), *d)
    tt = lambda out, x, y, o, *d: op("v", lambda e: e.tensor_tensor(out, x, y, o), *d)
    cp = lambda out, x, *d: op("v", lambda e: e.tensor_copy(out, x), *d)
    red = lambda out, x, o, *d: op("v", lambda e: e.tensor_reduce(out, x, AxisListType.X, o), *d)
    scan = lambda out, x, y, i, o, *d: op("v", lambda e: e.tensor_tensor_scan(out, x, y, i, OP.add, o), *d)
    quant = lambda q, s, x, *d: op("v", lambda e: e.quantize_mx(q, s, x), *d)
    act = lambda out, x, f, b, s, *d: op("a", lambda e: e.activation(out, x, f, bias=b, scale=s), *d)
    acc = lambda out, x, f, b, o, *d: op("a", lambda e: e.activation(out, x, f, bias=b, scale=1.0, accum_out=o), *d)
    pickq = lambda out, win, off, *d: op("v", lambda e: e.tensor_copy(out.bitcast(u32), win.bitcast(u32).indirect(off)), *d)
    picks = lambda out, win, off, *d: op("a", lambda e: e.activation(out, win.indirect(off), AF.Copy), *d)
    quad = lambda q: slice(32 * q, 32 * q + 32)
    bank = lambda k, n: T.ps[:, 512 * k:512 * k + n]

    def mm(out, w, ws, x, xs, start, stop, *d):
        return op("t", lambda e: e.matmul_mx(out, w, ws, x, xs, start, stop), *d)

    d_rt = dma("a", "drt", T.rtt[:, 0:16], T.rt[:, 0:16])
    d_x = dma("s", "dx", T.xt[:, 0:768], T.x[:])
    d_w = dma("s", "dw", T.wt[:], T.w[:], d_x)
    d_r2 = dma("s", "dr2", T.r2t[:, 0:20], T.r2[:, 0:20])
    d_vx = dma("s", "dvx", T.vxt[:], T.vx[:])
    d_vh = dma("s", "dvh", T.vht[:], T.vh[:])

    gi = lambda out, pat, cmul: op("g", lambda e: e.iota(out, pat, 0, cmul))
    gi(T.pI[:], [[0, 16]], 1)
    gi(T.b16[:], [[16, 8]], 0)
    k_g = gi(T.b32[:], [[32, 8]], 0)
    k_fin = gi(T.bfin[:], [[64, 4], [16, 2]], 0)
    k_80 = op("g", lambda e: e.iota(T.i80[:], [[1, 80]], 0, 0, allow_small_or_imprecise_dtypes=True))
    ms(T.rtt[:, 32:512], 0.0)
    for c in range(len(RTB)):
        k_rto = ms(T.rto[:, 2 * c:2 * c + 2], RTB[c])
    k_x0 = ms(T.xt[:, 768:776], 0.0)
    ms(T.th1[0:64, :], -EPS / 2)
    ms(T.th1[64:128, :], EPS / 2)
    ms(T.eb1[0:32, :], 0.0)
    ms(T.eb1[32:64, :], -EPS)
    ms(T.eb1[64:96, :], EPS)
    k_th = ms(T.eb1[96:128, :], 0.0)
    ms(T.zb[:], 0.0)
    k_jk = ms(T.jkd[:, 192:193], -192.0)
    k_jk = ms(T.jkd[:, 448:449], -192.0)
    kr = ts(T.rI[:], T.pI[:], 15, None, OP.bitwise_and, None, k_g)
    kq = ts(T.qI[:], T.pI[:], 31, None, OP.bitwise_and, None)
    k1 = tt(T.cs[:], T.rI[:, 0:8], T.b16[:], OP.add, kr)
    ts(T.csp[:], T.cs[:], 0.5, None, OP.add, None, k1)
    k_cs = ts(T.csn[:], T.cs[:], -1.0, -0.5, OP.mult, OP.add)
    k_lw = ms(T.lwho[:], -1.0)
    k_mi = ms(T.msgi[:, 8 * rank:8 * rank + 8], 0.0)
    k_mo = ms(T.msgo[:], 0.0)

    k = ts(T.rtt[:, 16:32], T.rtt[:, 0:16], -1.0, None, OP.mult, None, d_rt)
    k_rq = quant(T.rtq[:], T.rts[:], T.rtt[:], k)
    kp1 = pickq(T.rpq[:, 0:256], T.rtq[:], T.rto[:, 0:16], k_rq)
    ks1 = picks(T.rps[:, 0:256], T.rts[:], T.rto[:, 0:16], k_rq, k_rto)
    k_xq = quant(T.xq[:], T.xs[:], T.xt[:], d_x, k_x0)
    kp2 = pickq(T.rpq[:, 256:448], T.rtq[:], T.rto[:, 16:28])
    ks2 = picks(T.rps[:, 256:448], T.rts[:], T.rto[:, 16:28])
    dm = []
    for j in range(3):
        mm(bank(j, 192), T.rpq[:, 0:128], T.rps[:, 0:128], T.xq[:, 0:192], T.xs[:, 0:192], True, False, kp1, ks1, k_xq)
        a = 32 * RTS[j]
        dj = (kp2, ks2) if j else ()
        dm.append(mm(bank(j, 192), T.rpq[:, a:a + 128], T.rps[:, a:a + 128], T.xq[:, 0:192], T.xs[:, 0:192], False, True, *dj))
    k_z1 = act(T.z1[:], bank(0, 192), AF.Identity, T.eb1[:], 1.0, dm[0], k_th)
    k2 = tt(T.cm[:], T.qI[:, 0:8], T.b32[:], OP.add, kq)
    k_cm = ts(T.cmn[:], T.cm[:], -1.0, -0.5, OP.mult, OP.add, k2)
    k = tt(T.z2[:], bank(1, 192), T.z1[:], OP.min, dm[1], k_z1)
    k_d1 = tt(T.z3[:], bank(2, 192), T.z2[:], OP.min, dm[2], k)
    k = ts(T.mk[:], T.z3[:], T.th1[:], None, OP.is_gt, None, k_d1)
    k_cum = scan(T.cum[:], T.mk[:], T.zb[:, 0:192], 0.0, OP.add, k)
    k_a = [acc(T.jka[:, 192 * c:192 * c + 192], T.cum[:], AF.Sign, T.csn[:, c:c + 1], T.cnt1[:, c:c + 1], k_cum, k_cs) for c in range(3)]
    k3 = ts(T.jkd[:, 0:192], T.cum[:], T.csp[:, 3:4], 2.0, OP.is_gt, OP.mult, k_cum)
    k4 = ts(T.jkd[:, 256:448], T.cum[:], T.csp[:, 4:5], 2.0, OP.is_gt, OP.mult)
    ts(T.cnt1[:, 5:6], T.cum[:, 191:192], -2.0, 192.0, OP.mult, OP.add)
    red(T.cnt1[:, 3:4], T.jkd[:, 0:193], OP.add, k3, k_jk)
    k_c = red(T.cnt1[:, 4:5], T.jkd[:, 256:449], OP.add, k4)
    pk, psc, k_off = {}, {}, {}
    for i, b in enumerate(order + [rank]):
        for q in range(N):
            k_off[b] = ts(T.off1[quad(q), 6 * b:6 * b + 6], T.cnt1[quad(b), 0:6], -0.5, 96.0, OP.mult, OP.add, k_c, k_a[-1])
        o, so = (T.sl1[:, 80 * i:80 * i + 80], T.ss1[:, 80 * i:80 * i + 80]) if b != rank else \
                (T.land1[:, 80 * b:80 * b + 80], T.lans1[:, 80 * b:80 * b + 80])
        pk[b] = pickq(o, T.xq[:, 0:194], T.off1[:, 6 * b:6 * b + 5], k_off[b])
        psc[b] = picks(so, T.xs[:, 0:194], T.off1[:, 6 * b:6 * b + 5], k_off[b])
        if b != rank:
            send(b, c8(T.land1[:, 80 * rank:80 * rank + 80]), c8(T.sl1[:, 80 * i:80 * i + 80]), "arr%d" % rank, pk[b], k_lw)
            send(b, T.lans1[:, 80 * rank:80 * rank + 80], T.ss1[:, 80 * i:80 * i + 80], "arr%d" % rank, psc[b])
    k_m = [acc(T.jka[:, 576 + 192 * c:768 + 192 * c], T.cum[:], AF.Sign, T.cmn[:, c:c + 1], T.cntm[:, c:c + 1], k_cm) for c in range(3)]
    m_v, m_a = {}, {}
    for b in order + [rank]:
        m, o = (T.msgo, 8 * b) if b != rank else (T.msgi, 8 * rank)
        m_v[b] = cp(m[:, o + 1:o + 2], T.off1[:, 6 * b + 5:6 * b + 6], k_off[b], k_mo)
        for c in range(3):
            m_a[b] = act(m[quad(c), o:o + 1], T.cntm[quad(b), c:c + 1], AF.Copy, 96.0, -0.5, k_m[2], k_mo)
        if b != rank:
            send(b, T.msgi[:, 8 * rank:8 * rank + 2], T.msgo[:, o:o + 2], "am", m_v[b], m_a[b])

    k_oz = ms(T.ozero[:], TOK)
    k_z = pickq(T.land1[:, NX:XC], T.xq[:, 0:194], T.ozero[:, 0:1], k_xq, k_oz)
    k_zs = picks(T.lans1[:, NX:XC], T.xs[:, 0:194], T.ozero[:, 0:1], k_z)
    k_wq = quant(T.wq[:], T.wsc[:], T.wt[:], d_w)
    ms(T.r2t[:, 40:512], 0.0)
    k = ts(T.r2t[:, 20:40], T.r2t[:, 0:20], -1.0, None, OP.mult, None, d_r2)
    k_r2q = quant(T.r2q[:], T.r2s[:], T.r2t[:], k)
    srt = sorted(others)
    one = {srt[0]: srt[1], srt[1]: srt[0], srt[2]: srt[0], rank: 0}
    two = {srt[0]: srt[2], srt[1]: srt[2], srt[2]: srt[1], rank: 0}
    blocks = [0, 1, 2, 3] + [5 + one[q] for q in range(N)] + [5 + two[q] for q in range(N)] + [4] * 4
    for c in range(16):
        k_o = ms(T.r2o[:, 2 * c:2 * c + 2], blocks[c])
    k_r2p = pickq(T.r2p[:], T.r2q[:], T.r2o[:], k_o, k_r2q)
    k_r2s = picks(T.r2ps[:], T.r2s[:], T.r2o[:], k_o, k_r2q)
    k_z2 = pickq(T.land2[:, 64 * rank:64 * rank + 64], T.xq[:, 0:194], T.ozero[:], k_xq)
    k_z2s = picks(T.lans2[:, 64 * rank:64 * rank + 64], T.xs[:, 0:194], T.ozero[:], k_z2)
    k_vx = quant(T.vxq[:], T.vxs[:], T.vxt[:], d_vx)
    k_vh = quant(T.vhq[:], T.vhs[:], T.vht[:], d_vh)
    for q in range(N):
        ms(T.th2[quad(q), :], -EPS / 2 if q == srt[2] else EPS / 2)
        k_t2 = ms(T.eb2[quad(q), :], -EPS if q == srt[1] else 0.0)
    ms(T.zf[:], 0.0)
    ms(T.cap[:], 64 * STEP)
    k_je = ms(T.jke[:, 320:321], -320.0)
    k_num = ms(T.num[:], -1.0)
    k = ts(T.ofi[:], T.bfin[:], 32.0, None, OP.add, None, k_fin)
    k = tt(T.ofi[:], T.rI[:, 0:8], T.ofi[:], OP.add, k)
    k_ofin = cp(T.ofin[:], T.ofi[:], k)

    arr = lambda s: ("arr%d" % s, arrivals([s], 2))
    home = (pk[rank], psc[rank])
    halves = [(0, NH, [0, 1]), (NH, NX + 2, [2, 3])]
    W = []
    for h, (c0, c1, who) in enumerate(halves):
        deps = [arr(s) for s in who if s != rank] + list(home) + [k_z, k_zs, k_wq, k_d1, k_z1]
        W.append([mm(bank(4 * h + i, c1 - c0), T.wq[:, 128 * i:128 * i + 128], T.wsc[:, 128 * i:128 * i + 128], T.land1[:, c0:c1], T.lans1[:, c0:c1], True, True, *deps) for i in range(4)])
    kq_h = []
    for h, (c0, c1, who) in enumerate(halves):
        hv = lambda i: T.hb[:, 4 * c0 + i:4 * c1:4]
        k0 = act(hv(0), bank(4 * h, c1 - c0), AF.Relu, 0.0, 0.0625, W[h][0])
        k1 = ts(hv(1), bank(4 * h + 1, c1 - c0), 0.0, 0.0625, OP.max, OP.mult, W[h][1])
        k2 = act(hv(2), bank(4 * h + 2, c1 - c0), AF.Relu, 0.0, 0.0625, W[h][2])
        k3 = ts(hv(3), bank(4 * h + 3, c1 - c0), 0.0, 0.0625, OP.max, OP.mult, W[h][3])
        kq_h.append(quant(T.xw[:, HB + c0:HB + c1], T.xws[:, HB + c0:HB + c1], T.hb[:, 4 * c0:4 * c1], k0, k1, k2, k3))
    alla = [arr(s) for s in range(N) if s != rank]
    dma("s", "dxw", c8(T.xw[:, 0:XC]), c8(T.land1[:]), *alla, *home, k_z, k_zs)
    d_xw = dma("s", "dxw", T.xws[:, 0:XC], T.lans1[:])
    am = ("am", arrivals(others, 1))
    for s in range(N):
        d_nb = dma("s", "dnb", T.nb[0:1, 80 * s:80 * s + 80], T.msgi[0:80, 8 * s:8 * s + 1], am, m_v[rank], m_a[rank])

    H = lambda a, b: (T.xw[:, HB + a:HB + b], T.xws[:, HB + a:HB + b])
    P = lambda k: (T.r2p[:, 128 * k:128 * k + 128], T.r2ps[:, 128 * k:128 * k + 128])
    ea = mm(bank(0, NH), *P(3), *H(0, NH), True, True, kq_h[0], k_r2p, k_r2s, k_r2q)
    e0 = mm(bank(1, 128), *H(0, 128), T.r2q[:], T.r2s[:], True, True)
    mm(bank(2, NH), *P(0), *H(0, NH), True, False)
    fa = mm(bank(2, NH), *P(1), *H(0, NH), False, True)
    eb = mm(bank(4, NH), *P(3), *H(NH, NX), True, True, kq_h[1])
    e1 = mm(bank(5, 128), *H(128, 256), T.r2q[:], T.r2s[:], True, True)
    e2 = mm(bank(6, 128), *H(192, 320), T.r2q[:], T.r2s[:], True, True)
    mm(bank(7, NH), *P(0), *H(NH, NX), True, False)
    fb = mm(bank(7, NH), *P(1), *H(NH, NX), False, True)
    mm(bank(3, NX), *P(0), *H(0, NX), True, False)
    f2 = mm(bank(3, NX), *P(2), *H(0, NX), False, True)
    e4 = lambda k: T.ps[:, 512 * k + 4:512 * k + 5]
    ken0 = act(T.en[:, 0:1], e4(1), AF.Copy, 0.0, 1.0, e0)
    act(T.y1[:, 0:NH], bank(2, NH), AF.Identity, T.eb2[:], 1.0, fa, k_t2)
    ken1 = act(T.en[:, 1:2], e4(5), AF.Copy, 0.0, 1.0, e1)
    ken2 = act(T.en[:, 2:3], e4(6), AF.Copy, 0.0, 1.0, e2)
    k_y1 = act(T.y1[:, NH:NX], bank(7, NH), AF.Identity, T.eb2[:], 1.0, fb)
    for s in range(N):
        ki = ts(T.inv[:, 80 * s:80 * s + 80], T.i80[:], T.msgi[:, 8 * s + 1:8 * s + 2], BIG, OP.is_ge, OP.mult, k_80, am, m_v[rank])
    tt(T.em[:, 0:NH], bank(0, NH), T.inv[:, 0:NH], OP.add, ea, ki)
    k_em = tt(T.em[:, NH:NX], bank(4, NH), T.inv[:, NH:NX], OP.add, eb)
    kc0 = ts(T.jk2[:, 0:320], T.em[:], T.en[:, 0:1], None, OP.is_lt, None, k_em, ken0)
    kc1 = ts(T.jk2[:, 320:640], T.em[:], T.en[:, 1:2], None, OP.is_lt, None, ken1)
    k = act(T.jk2[:, 640:960], T.em[:], AF.Sign, T.en[:, 2:3], -1.0, k_em, ken2)
    kl0 = acc(T.jkb[:, 0:320], T.jk2[:, 0:320], AF.Copy, 0.0, T.lt[:, 0:1], kc0)
    kl2 = acc(T.jkb[:, 320:640], T.jk2[:, 640:960], AF.Relu, 0.0, T.lt[:, 2:3], k)
    kl1 = red(T.lt[:, 1:2], T.jk2[:, 320:640], OP.add, kc1)
    k_y2 = tt(T.y2[:], bank(3, NX), T.y1[:], OP.min, f2, k_y1)
    k = act(T.sn[:], T.y2[:], AF.Sign, T.th2[:], 1.0, k_y2)
    k_ns = act(T.ns[:], T.sn[:], AF.Relu, 0.0, -BIG, k)
    for s in range(N):
        k_n = act(T.num[0:1, 80 * s:80 * s + 80], T.nb[0:1, 80 * s:80 * s + 80], AF.Copy, float(TOK * s), 1.0, d_nb, k_num)
    kp = ts(T.pen[:, 0:3], T.lt[:, 0:3], DF - 0.5, LOW, OP.is_ge, OP.mult, kl0, kl1, kl2)
    for k in range(3):
        ts(T.bc[:, 32 * k:32 * k + 32], T.zf[:], T.en[:, k:k + 1], T.pen[:, k:k + 1], OP.add, OP.add, kp)
        kc = ts(T.bc[:, 96 + 32 * k:128 + 32 * k], T.zf[:], T.lt[:, k:k + 1], T.pen[:, k:k + 1], OP.add, OP.add)
    kc = op("v", lambda e: e.transpose(T.bt[:], T.bc[:]), kc)
    k_eb = tt(T.emb[:], T.em[:], T.ns[:], OP.add, k_ns)
    red(T.qm[:, 0:1], T.bt[:, 0:96], OP.max, kc)
    kc = red(T.qm[:, 1:2], T.bt[:, 96:192], OP.max)
    tt(T.g4[0:64, :], T.qm[0:64, :], T.qm[64:128, :], OP.max, kc)
    kc = tt(T.g4[64:128, :], T.qm[64:128, :], T.qm[0:64, :], OP.max)
    for q in range(N):
        k = tt(T.tl[quad(q), :], T.g4[quad(q), :], T.g4[quad(q ^ 1), :], OP.max, kc)
    k_sg = act(T.sg[:], T.emb[:], AF.Sign, T.tl[:, 0:1], -1.0, k, k_eb)
    k_gd = ts(T.gd[:], T.em[:], T.tl[:, 0:1], STEP, OP.is_equal, OP.mult, k)
    k_i = ts(T.ini[:], T.tl[:, 1:2], DF + 0.5, STEP, OP.subtract, OP.mult)
    k = scan(T.nq[:], T.gd[:], T.cap[:], T.ini[:], OP.min, k_i)
    k = tt(T.mk2[:], T.sg[:], T.nq[:], OP.is_gt, k, k_sg)
    k_c2 = scan(T.cum2[:], T.mk2[:], T.zb[:], 0.0, OP.add, k)
    ka = acc(T.jkb[:, 640:960], T.cum2[:], AF.Sign, T.csn[:, 0:1], T.cnt2[:, 0:1], k_c2)
    k = ts(T.jke[:, 0:320], T.cum2[:], T.csp[:, 1:2], 2.0, OP.is_gt, OP.mult, k_c2)
    k = red(T.cnt2[:, 1:2], T.jke[:, 0:321], OP.add, k)
    kc = ts(T.cnt2[:, 2:4], T.cnt2[:, 0:2], -2.0 * HB, None, OP.add, None, k, ka)
    for i, b in enumerate(order):
        for q in range(N):
            ko = ts(T.off2[quad(q), 4 * i:4 * i + 4], T.cnt2[quad(b), 0:4], -0.5, NX / 2.0, OP.mult, OP.add, kc)
        o = slice(64 * i, 64 * i + 64)
        kk = pickq(T.sl2[:, o], T.xw[:], T.off2[:, 4 * i:4 * i + 4], ko, d_xw)
        ks = picks(T.ss2[:, o], T.xws[:], T.off2[:, 4 * i:4 * i + 4], ko, d_xw)
        d = slice(64 * rank, 64 * rank + 64)
        send(b, c8(T.land2[:, d]), c8(T.sl2[:, o]), "arrb", kk)
        send(b, T.lans2[:, d], T.ss2[:, o], "arrb", ks)
    for i in range(3):
        kw = op("a", lambda e: e.activation(T.wg[:, 32 * i:32 * i + 32], T.num[:].indirect(T.off2[:, 4 * i:4 * i + 2]), AF.Copy), k_n)
    kw = op("v", lambda e: e.transpose(T.wtr[:], T.wg[:]), kw)
    for i, b in enumerate(order):
        send(b, T.lwho[:, rank:rank + 1], T.wtr[:, 32 * i:32 * i + 1], "aw", kw)

    ab = ("arrb", arrivals(others, 2))
    mm(bank(5, 224), T.vxq[:], T.vxs[:], T.land2[:, 0:224], T.lans2[:, 0:224], True, False, ab, k_z2, k_z2s, k_vx, k_vh, ken1)
    ty = mm(bank(5, 224), T.vhq[:], T.vhs[:], T.land2[:, 32:256], T.lans2[:, 32:256], False, True)
    kf = pickq(T.fin[:], T.land2[:], T.ofin[:], ab, k_ofin)
    kfs = picks(T.fins[:], T.lans2[:], T.ofin[:], ab, k_ofin)
    for a in range(N):
        ky = cp(T.ys[:, CB * a:CB * a + CB], T.ps[:, 2560 + 64 * a:2560 + 64 * a + CB], ty)
    dma("s", "dout", T.oc[:], c8(T.fin[:]), kf)
    for k in range(4):
        dma("s" if k < 2 else "a", "dout", T.osc[4 * k:4 * k + 4, :], T.fins[32 * k:32 * k + 4, :], kfs)
    dma("a", "dout", T.y[:], T.ys[:], ky)
    kw = op("v", lambda e: e.transpose(T.whot[:], T.lwho[:]), ("aw", arrivals(others, 1)), k_lw)
    dma("s", "dout", T.who[:], T.whot[0:4, :], kw)
    wait("g", [(s, n) for s, n in tot.items()])
